import numpy as np
import ml_dtypes


def mxq(x, axis, fmt="e4m3"):
    dtype, down = {"e4m3": (ml_dtypes.float8_e4m3fn, 7), "e5m2": (ml_dtypes.float8_e5m2, 14)}[fmt]
    v = np.moveaxis(np.asarray(x, np.float32).astype(ml_dtypes.bfloat16).astype(np.float64), axis, -1)
    blocks = v.reshape(v.shape[:-1] + (-1, 32))
    amax = np.abs(blocks).max(-1, keepdims=True)
    byte = np.maximum(np.where(amax > 0, np.frexp(amax)[1] - 1 + 127, 0) - down, 1)
    scale = np.exp2(byte - 127.0)
    codes = (blocks / scale).astype(np.float32).astype(dtype).astype(np.float64)
    return np.moveaxis((codes * scale).reshape(v.shape), -1, axis)


WIDE = False


def mx_kscale(k):
    if not WIDE:
        return np.ones(k)
    levels = np.array([10, -10, 5, -5, 0])
    if k % 512:
        return np.exp2(np.random.permutation(np.resize(levels, k // 32))).repeat(32)
    a = np.empty((k // 512, 16))
    for p in range(k // 512):
        a[p, :8] = np.random.permutation(np.resize(levels, 8))
        for g in range(8):
            far = levels[np.abs(levels - a[p, g]) >= 10]
            a[p, g + 8] = far[np.random.randint(len(far))]
    return np.exp2(a.ravel()).repeat(32)


def f64(x):
    return np.asarray(x).astype(np.float64)


def striped(idx):
    return np.tile(idx.reshape(-1, 16).T, (8, 1)).astype(np.uint16)


def unstriped(offs):
    return offs[:16].T.reshape(-1).astype(np.int64)


def pack_weight(w):
    k, n = w.shape
    w = f64(np.asarray(w, np.float32).astype(ml_dtypes.bfloat16)).reshape(k // 32, 32, n)
    amax = np.abs(w).max(1)
    byte = np.clip(np.where(amax > 0, np.frexp(amax)[1] - 1 + 127 - 7, 1), 1, 254)
    scaled = (w * np.exp2(127.0 - byte)[:, None, :]).reshape(k, n).astype(np.float32)
    words = np.ascontiguousarray(scaled.reshape(k // 512, 128, 4, n).transpose(0, 1, 3, 2)).astype(ml_dtypes.float8_e4m3fn).view(np.uint8)
    return words, np.ascontiguousarray(byte.astype(np.uint8).reshape(k // 512, 16, n))


def unpack_weight(words, scales):
    g, p, n, _ = words.shape
    vals = np.ascontiguousarray(words).view(ml_dtypes.float8_e4m3fn).astype(np.float64) * np.repeat(np.exp2(scales.astype(np.float64) - 127.0), 8, axis=1)[..., None]
    return vals.transpose(0, 1, 3, 2).reshape(g * 512, n)


E2M1 = np.array([0.0, 0.5, 1.0, 1.5, 2.0, 3.0, 4.0, 6.0, -0.0, -0.5, -1.0, -1.5, -2.0, -3.0, -4.0, -6.0])


def pack_fp4(w):
    k, n = w.shape
    w = f64(np.asarray(w, np.float32).astype(ml_dtypes.bfloat16)).reshape(k // 32, 32, n)
    amax = np.abs(w).max(1)
    mant, ex = np.frexp(amax / 6.0)
    byte = np.clip(np.where(amax > 0, np.where(mant > 0.5, ex, ex - 1) + 127, 1), 1, 254)
    scaled = (w * np.exp2(127.0 - byte)[:, None, :]).reshape(k, n).astype(np.float32)
    c = np.ascontiguousarray(scaled.reshape(k // 512, 128, 4, n).transpose(0, 1, 3, 2)).astype(ml_dtypes.float4_e2m1fn).view(np.uint8) & 0xF
    words = (c[..., 0::2] | (c[..., 1::2] << 4)).reshape(k // 512, 128, 2 * n)
    return np.ascontiguousarray(words), np.ascontiguousarray(byte.astype(np.uint8).reshape(k // 512, 16, n))


def unpack_fp4(words, scales):
    g, _, n = scales.shape
    words = np.ascontiguousarray(words).reshape(g, 128, n, 2)
    nib = np.empty((g, 128, n, 4), np.uint8)
    nib[..., 0::2] = words & 0xF
    nib[..., 1::2] = words >> 4
    vals = E2M1[nib] * np.repeat(np.exp2(scales.astype(np.float64) - 127.0), 8, axis=1)[..., None]
    return vals.transpose(0, 1, 3, 2).reshape(g * 512, n)


def planes(y):
    n, m = y.shape
    v = y.astype(np.float32).astype(ml_dtypes.bfloat16).astype(np.float64).reshape(n // 32, 32, m)
    top = np.abs(v).max(1)
    byte = np.clip(np.where(top > 0, np.frexp(top)[1] - 1 + 127 - 7, 1), 1, 254)
    codes = (v * np.exp2(127.0 - byte)[:, None, :]).reshape(n, m).astype(np.float32).astype(ml_dtypes.float8_e4m3fn).view(np.uint8)
    words = codes.reshape(n // 512, 128, 4, m).transpose(0, 1, 3, 2)
    return np.ascontiguousarray(words), np.ascontiguousarray(byte.astype(np.uint8).reshape(n // 512, 16, m))


K, T, S, H, N = 512, 2048, 512, 512, 512


def setup_inputs():
    n = np.random.standard_normal
    s = mx_kscale(K)[:, None]
    u = mx_kscale(H)
    packed_xT = pack_weight(n((K, T)) * s)
    packed_w3 = pack_fp4(n((H, N)) / np.sqrt(H) / u[:, None])
    packed_w4 = pack_fp4(n((K, N)) / np.sqrt(K) / s)
    return {
        "x_words": packed_xT[0],
        "x_scales": packed_xT[1],
        "w1": (n((K, H)) / np.sqrt(2 * K) / s * u).astype(np.float32),
        "w2": (n((K, H)) / np.sqrt(2 * K) / s * u).astype(np.float32),
        "w3_words": packed_w3[0],
        "w3_scales": packed_w3[1],
        "w4_words": packed_w4[0],
        "w4_scales": packed_w4[1],
        "offs": striped(np.random.permutation(T)[:S]),
        "dst": striped(np.random.permutation(T)[:S]),
    }


def reference(x_words, x_scales, w1, w2, w3_words, w3_scales, w4_words, w4_scales, offs, dst):
    xq = unpack_weight(x_words, x_scales)[:, unstriped(offs)]
    x_dst = unpack_weight(x_words, x_scales)[:, unstriped(dst)]
    y = mxq(f64(w1), 0, "e4m3").T @ xq + mxq(f64(w2), 0, "e4m3").T @ x_dst
    h = np.maximum(y, 0.2 * y)
    e = np.exp(unpack_fp4(w3_words, w3_scales).T @ mxq(h, 0, "e4m3"))
    v = unpack_fp4(w4_words, w4_scales).T @ xq
    out_0 = e * v
    return (out_0,) + planes(out_0)

@@ -1,0 +1,224 @@
+from contextlib import ExitStack
+
+import concourse.mybir as mybir
+
+K, T, S, H, N = 512, 2048, 512, 512, 512
+FLOPS = 2 * (2 * K * H * S + H * N * S + K * N * S)
+
+F32 = mybir.dt.float32
+BF16 = mybir.dt.bfloat16
+I32 = mybir.dt.int32
+U32 = mybir.dt.uint32
+U16 = mybir.dt.uint16
+U8 = mybir.dt.uint8
+FP8X4 = mybir.dt.float8_e4m3fn_x4
+FP4X4 = mybir.dt.float4_e2m1fn_x4
+ACT = mybir.ActivationFunctionType
+ALU = mybir.AluOpType
+
+P = 128
+PACK = 4
+CH = 128
+NCH = S // CH
+SLOPE = 0.2
+
+
+def tile_picked_zgatt_exp_po_kernel(
+    tc, x_words, x_scales, w1, w2, w3_words, w3_scales, w4_words, w4_scales, offs, dst, out_0, out_1, out_2
+):
+    nc = tc.nc
+    with ExitStack() as ctx:
+        keep = ctx.enter_context(tc.tile_pool(name="keep", bufs=1))
+        shared = ctx.enter_context(tc.tile_pool(name="shared", bufs=1))
+        psum = ctx.enter_context(tc.psum_pool(name="psum", bufs=1))
+
+        def sb(name, shape, dtype, tag=None):
+            return keep.tile(shape, dtype, name=name, tag=tag or name, align_bytes=64)
+
+        xs_tab = sb("xs_tab", [P, T], U8)
+        ws_raw = shared.tile([P, 2 * N], U8, name="ws_raw", align_bytes=64, offset=0)
+        nc.vector.memset(ws_raw[:].bitcast(I32), 0)
+        nc.vector.memset(xs_tab[:].bitcast(I32), 0)
+        warm_in = sb("warm_in", [P, 1], F32)
+        warm_out = sb("warm_out", [P, 1], F32)
+        nc.vector.memset(warm_in[:], 0.0)
+
+        w4_raw = sb("w4_raw", [P, 2 * N], U8, tag="first")
+        w3_raw = sb("w3_raw", [P, 2 * N], U8, tag="second")
+        nc.sync.dma_start(out=w4_raw[:].bitcast(I32), in_=w4_words[0].bitcast(I32))
+        nc.sync.dma_start(out=w3_raw[:].bitcast(I32), in_=w3_words[0].bitcast(I32))
+        offs_t = sb("offs_t", [P, S // 16], U16)
+        dst_t = sb("dst_t", [P, S // 16], U16)
+        nc.sync.dma_start(offs_t[:], offs)
+        nc.sync.dma_start(dst_t[:], dst)
+        w1_raw = sb("w1_raw", [P, PACK, H], F32)
+        nc.sync.dma_start(out=w1_raw[:], in_=w1.rearrange("(p j) c -> p j c", j=PACK))
+        xw_tab = sb("xw_tab", [P, T], U32)
+        nc.sync.dma_start(out=xw_tab[:].bitcast(I32), in_=x_words[0].rearrange("p n t -> p (n t)").bitcast(I32))
+        nc.scalar.dma_start(out=ws_raw[0:P:8, 0:N].bitcast(I32), in_=w4_scales[0].bitcast(I32))
+        nc.scalar.dma_start(out=ws_raw[0:P:8, N : 2 * N].bitcast(I32), in_=w3_scales[0].bitcast(I32))
+        for q in range(4):
+            nc.scalar.dma_start(
+                out=xs_tab[32 * q : 32 * q + 4, :].bitcast(I32), in_=x_scales[0, 4 * q : 4 * q + 4, :].bitcast(I32)
+            )
+        nc.scalar.activation(out=warm_out[:], in_=warm_in[:], func=ACT.Exp)
+
+        w4_q = sb("w4_q", [P, 2 * N], U8)
+        w3_q = sb("w3_q", [P, 2 * N], U8)
+        ws_q = sb("ws_q", [P, 2 * N], U8)
+        for dealt, raw in ((w4_q, w4_raw), (w3_q, w3_raw)):
+            nc.vector.tensor_copy(
+                out=dealt[:].rearrange("p (t m b) -> p t m b", t=PACK, b=2),
+                in_=raw[:].rearrange("p (m t b) -> p t m b", t=PACK, b=2),
+            )
+        w2_view = w2.rearrange("(p j) c -> p j c", j=PACK)
+        w2_raw = []
+        for h in range(2):
+            piece = sb("w2_raw%d" % h, [P, PACK, H // 2], F32, tag=("first", "second")[h])
+            nc.sync.dma_start(out=piece[:], in_=w2_view[:, :, h * (H // 2) : (h + 1) * (H // 2)])
+            w2_raw.append(piece)
+        nc.vector.tensor_copy(
+            out=ws_q[:].rearrange("p (w t m) -> p w t m", w=2, t=PACK),
+            in_=ws_raw[:].rearrange("p (w m t) -> p w t m", w=2, t=PACK),
+        )
+        for r in range(1, 4):
+            nc.scalar.dma_start(out=ws_q[r:P:32, :].bitcast(I32), in_=ws_q[8 * r : P : 32, :].bitcast(I32))
+
+        src_s = shared.tile([P, S], U8, name="src_s", align_bytes=64, offset=0)
+        dst_s = shared.tile([P, S], U8, name="dst_s", align_bytes=64, offset=S)
+        src_w = sb("src_w", [P, S], U32)
+        dst_w = sb("dst_w", [P, S], U32)
+        nc.vector.tensor_copy(src_s[:], xs_tab[:].indirect(offs_t[:]))
+        nc.vector.tensor_copy(dst_s[:], xs_tab[:].indirect(dst_t[:]))
+
+        w1_b = sb("w1_b", [P, PACK * H], BF16)
+        w1_q = sb("w1_q", [P, H], U32)
+        w1_s = sb("w1_s", [P, H], U8)
+        nc.scalar.copy(
+            out=w1_b[:].rearrange("p (t m j) -> p m j t", t=PACK, j=PACK),
+            in_=w1_raw[:].rearrange("p j (m t) -> p m j t", t=PACK),
+        )
+        nc.vector.tensor_copy(src_w[:], xw_tab[:].indirect(offs_t[:]))
+        nc.vector.tensor_copy(dst_w[:], xw_tab[:].indirect(dst_t[:]))
+        nc.vector.quantize_mx(out=w1_q[:].bitcast(FP8X4), scales=w1_s[:], in_=w1_b[:])
+
+        v_ps = [psum.tile([P, PACK, CH], F32, name="v_ps%d" % c) for c in range(NCH)]
+        for c in range(NCH):
+            cols = slice(c * CH, (c + 1) * CH)
+            for t in range(PACK):
+                nc.tensor.matmul_mx(
+                    out=v_ps[c][:, t, :],
+                    lhsT=w4_q[:, 2 * P * t : 2 * P * (t + 1)].bitcast(FP4X4),
+                    lhsT_scale=ws_q[:, P * t : P * (t + 1)],
+                    rhs=src_w[:, cols].bitcast(FP8X4),
+                    rhs_scale=src_s[:, cols],
+                    start=True,
+                    stop=True,
+                )
+
+        w2_b = sb("w2_b", [P, PACK * H], BF16)
+        w2_q = sb("w2_q", [P, H], U32)
+        w2_s = sb("w2_s", [P, H], U8)
+        HM = P // 2
+        w2_bv = w2_b[:].rearrange("p (t m j) -> p m j t", t=PACK, j=PACK)
+
+        def quant_w2(h, t):
+            c0 = P * t + HM * h
+            nc.vector.quantize_mx(
+                out=w2_q[:, c0 : c0 + HM].bitcast(FP8X4),
+                scales=w2_s[:, c0 : c0 + HM],
+                in_=w2_b[:, PACK * c0 : PACK * (c0 + HM)],
+            )
+
+        raw0 = w2_raw[0][:].rearrange("p j (m t) -> p m j t", t=PACK)
+        raw1 = w2_raw[1][:].rearrange("p j (m t) -> p m j t", t=PACK)
+        nc.scalar.copy(out=w2_bv[:, 0:HM], in_=raw0)
+        for t in range(PACK):
+            quant_w2(0, t)
+        nc.vector.tensor_copy(out=w2_bv[:, HM:P, :, 0:2], in_=raw1[:, :, :, 0:2])
+        nc.scalar.copy(out=w2_bv[:, HM:P, :, 2:4], in_=raw1[:, :, :, 2:4])
+        for t in range(PACK):
+            quant_w2(1, t)
+
+        y_ps = [psum.tile([P, PACK, CH], F32, name="y_ps%d" % c) for c in range(NCH)]
+        small = [sb("small%d" % c, [P, CH * PACK], F32) for c in range(NCH)]
+        h_b = [sb("h_b%d" % c, [P, CH * PACK], BF16) for c in range(NCH)]
+        h_q = [sb("h_q%d" % c, [P, CH], U32) for c in range(NCH)]
+        h_s = [sb("h_s%d" % c, [P, CH], U8) for c in range(NCH)]
+        e_f = [sb("e_f%d" % c, [P, PACK, CH], F32) for c in range(NCH)]
+        o_f = [sb("o_f%d" % c, [P, PACK, CH], F32) for c in range(NCH)]
+        o_b = [sb("o_b%d" % c, [P, CH * PACK], BF16) for c in range(NCH)]
+        o_q = sb("o_q", [P, S], U32)
+        o_s = sb("o_s", [P, S], U8)
+        out_rows = out_0.rearrange("(p t) n -> p t n", t=PACK)
+        out_words = out_1[0].rearrange("p n t -> p (n t)").bitcast(I32)
+
+        def hidden_mm(c):
+            cols = slice(c * CH, (c + 1) * CH)
+            for t in range(PACK):
+                m = slice(P * t, P * (t + 1))
+                nc.tensor.matmul_mx(
+                    out=y_ps[c][:, t, :], lhsT=w1_q[:, m].bitcast(FP8X4), lhsT_scale=w1_s[:, m],
+                    rhs=src_w[:, cols].bitcast(FP8X4), rhs_scale=src_s[:, cols], start=True, stop=False,
+                )
+                nc.tensor.matmul_mx(
+                    out=y_ps[c][:, t, :], lhsT=w2_q[:, m].bitcast(FP8X4), lhsT_scale=w2_s[:, m],
+                    rhs=dst_w[:, cols].bitcast(FP8X4), rhs_scale=dst_s[:, cols], start=False, stop=True,
+                )
+
+        def leaky(c):
+            y_nt = y_ps[c][:].rearrange("p t n -> p n t")
+            nc.scalar.activation(
+                out=small[c][:].rearrange("p (n t) -> p n t", t=PACK), in_=y_nt, func=ACT.Copy, scale=SLOPE
+            )
+            nc.vector.tensor_tensor(
+                out=h_b[c][:].rearrange("p (n t) -> p n t", t=PACK),
+                in0=y_nt,
+                in1=small[c][:].rearrange("p (n t) -> p n t", t=PACK),
+                op=ALU.max,
+            )
+
+        def scores(c):
+            nc.vector.quantize_mx(out=h_q[c][:].bitcast(FP8X4), scales=h_s[c][:], in_=h_b[c][:])
+            for t in range(PACK):
+                nc.tensor.matmul_mx(
+                    out=y_ps[c][:, t, :],
+                    lhsT=w3_q[:, 2 * P * t : 2 * P * (t + 1)].bitcast(FP4X4),
+                    lhsT_scale=ws_q[:, N + P * t : N + P * (t + 1)],
+                    rhs=h_q[c][:].bitcast(FP8X4),
+                    rhs_scale=h_s[c][:],
+                    start=True,
+                    stop=True,
+                )
+            nc.scalar.activation(out=e_f[c][:], in_=y_ps[c][:], func=ACT.Exp)
+
+        def message(c):
+            nc.vector.tensor_tensor(out=o_f[c][:], in0=v_ps[c][:], in1=e_f[c][:], op=ALU.mult)
+            nc.sync.dma_start(out=out_rows[:, :, c * CH : (c + 1) * CH], in_=o_f[c][:])
+
+        def round_out(c):
+            dst_v = o_b[c][:].rearrange("p (n i t) -> p n t i", i=4, t=PACK)
+            src_v = o_f[c][:].rearrange("p t (n i) -> p n t i", i=4)
+            if c == NCH - 1:
+                nc.vector.tensor_copy(out=dst_v, in_=src_v)
+            else:
+                nc.scalar.copy(out=dst_v, in_=src_v)
+
+        def planes(c):
+            cols = slice(c * CH, (c + 1) * CH)
+            nc.vector.quantize_mx(out=o_q[:, cols].bitcast(FP8X4), scales=o_s[:, cols], in_=o_b[c][:])
+            nc.sync.dma_start(out=out_words[:, cols], in_=o_q[:, cols].bitcast(I32))
+
+        for c in range(NCH):
+            hidden_mm(c)
+        stages = (leaky, scores, message, round_out, planes)
+        lag = (0, 1, 3, 4, 5)
+        for step in range(NCH + lag[-1]):
+            for stage, d in zip(stages, lag):
+                if 0 <= step - d < NCH:
+                    stage(step - d)
+        for q in range(4):
+            queue = nc.scalar if q % 2 else nc.sync
+            queue.dma_start(
+                out=out_2[0, 4 * q : 4 * q + 4, :].bitcast(I32), in_=o_s[32 * q : 32 * q + 4, :].bitcast(I32)
+            )

@@ -35,72 +35,77 @@ def tile_picked_zgatt_exp_po_kernel(
         def sb(name, shape, dtype, tag=None):
             return keep.tile(shape, dtype, name=name, tag=tag or name, align_bytes=64)
 
+        def at(name, shape, dtype, offset):
+            return shared.tile(shape, dtype, name=name, align_bytes=64, offset=offset)
+
         xs_tab = sb("xs_tab", [P, T], U8)
-        ws_raw = shared.tile([P, 2 * N], U8, name="ws_raw", align_bytes=64, offset=0)
-        nc.vector.memset(ws_raw[:].bitcast(I32), 0)
+        w4s_raw = at("w4s_raw", [P, N], U8, 0)
+        w3s_raw = sb("w3s_raw", [P, N], U8)
         nc.vector.memset(xs_tab[:].bitcast(I32), 0)
+        nc.vector.memset(w4s_raw[:].bitcast(I32), 0)
+        nc.vector.memset(w3s_raw[:].bitcast(I32), 0)
         warm_in = sb("warm_in", [P, 1], F32)
         warm_out = sb("warm_out", [P, 1], F32)
         nc.vector.memset(warm_in[:], 0.0)
+        nc.scalar.activation(out=warm_out[:], in_=warm_in[:], func=ACT.Exp)
 
-        w4_raw = sb("w4_raw", [P, 2 * N], U8, tag="first")
-        w3_raw = sb("w3_raw", [P, 2 * N], U8, tag="second")
-        nc.sync.dma_start(out=w4_raw[:].bitcast(I32), in_=w4_words[0].bitcast(I32))
-        nc.sync.dma_start(out=w3_raw[:].bitcast(I32), in_=w3_words[0].bitcast(I32))
+        def load_scales(tile, rows, queue):
+            for q in range(4):
+                queue.dma_start(
+                    out=tile[32 * q : 32 * q + 4, :].bitcast(I32), in_=rows[0, 4 * q : 4 * q + 4, :].bitcast(I32)
+                )
+
+        def load_half(name, w, h):
+            piece = sb(name, [P, PACK, H // 2], F32)
+            view = w.rearrange("(p j) c -> p j c", j=PACK)
+            nc.sync.dma_start(out=piece[:], in_=view[:, :, h * (H // 2) : (h + 1) * (H // 2)])
+            return piece[:].rearrange("p j (m t) -> p m j t", t=PACK)
+
         offs_t = sb("offs_t", [P, S // 16], U16)
         dst_t = sb("dst_t", [P, S // 16], U16)
         nc.sync.dma_start(offs_t[:], offs)
         nc.sync.dma_start(dst_t[:], dst)
-        w1_raw = sb("w1_raw", [P, PACK, H], F32)
-        nc.sync.dma_start(out=w1_raw[:], in_=w1.rearrange("(p j) c -> p j c", j=PACK))
+        load_scales(xs_tab, x_scales, nc.sync)
         xw_tab = sb("xw_tab", [P, T], U32)
         nc.sync.dma_start(out=xw_tab[:].bitcast(I32), in_=x_words[0].rearrange("p n t -> p (n t)").bitcast(I32))
-        nc.scalar.dma_start(out=ws_raw[0:P:8, 0:N].bitcast(I32), in_=w4_scales[0].bitcast(I32))
-        nc.scalar.dma_start(out=ws_raw[0:P:8, N : 2 * N].bitcast(I32), in_=w3_scales[0].bitcast(I32))
-        for q in range(4):
-            nc.scalar.dma_start(
-                out=xs_tab[32 * q : 32 * q + 4, :].bitcast(I32), in_=x_scales[0, 4 * q : 4 * q + 4, :].bitcast(I32)
-            )
-        nc.scalar.activation(out=warm_out[:], in_=warm_in[:], func=ACT.Exp)
+        w1_raw = sb("w1_raw", [P, PACK, H], F32)
+        nc.sync.dma_start(out=w1_raw[:], in_=w1.rearrange("(p j) c -> p j c", j=PACK))
+        w4_raw = sb("w4_raw", [P, 2 * N], U8)
+        w3_raw = sb("w3_raw", [P, 2 * N], U8)
+        nc.sync.dma_start(out=w4_raw[:].bitcast(I32), in_=w4_words[0].bitcast(I32))
+        load_scales(w4s_raw, w4_scales, nc.sync)
+        w2_raw = [load_half("w2_raw%d" % h, w2, h) for h in range(2)]
+        nc.sync.dma_start(out=w3_raw[:].bitcast(I32), in_=w3_words[0].bitcast(I32))
+        load_scales(w3s_raw, w3_scales, nc.sync)
 
-        w4_q = sb("w4_q", [P, 2 * N], U8)
-        w3_q = sb("w3_q", [P, 2 * N], U8)
-        ws_q = sb("ws_q", [P, 2 * N], U8)
-        for dealt, raw in ((w4_q, w4_raw), (w3_q, w3_raw)):
-            nc.vector.tensor_copy(
-                out=dealt[:].rearrange("p (t m b) -> p t m b", t=PACK, b=2),
-                in_=raw[:].rearrange("p (m t b) -> p t m b", t=PACK, b=2),
-            )
-        w2_view = w2.rearrange("(p j) c -> p j c", j=PACK)
-        w2_raw = []
-        for h in range(2):
-            piece = sb("w2_raw%d" % h, [P, PACK, H // 2], F32, tag=("first", "second")[h])
-            nc.sync.dma_start(out=piece[:], in_=w2_view[:, :, h * (H // 2) : (h + 1) * (H // 2)])
-            w2_raw.append(piece)
-        nc.vector.tensor_copy(
-            out=ws_q[:].rearrange("p (w t m) -> p w t m", w=2, t=PACK),
-            in_=ws_raw[:].rearrange("p (w m t) -> p w t m", w=2, t=PACK),
-        )
-        for r in range(1, 4):
-            nc.scalar.dma_start(out=ws_q[r:P:32, :].bitcast(I32), in_=ws_q[8 * r : P : 32, :].bitcast(I32))
-
-        src_s = shared.tile([P, S], U8, name="src_s", align_bytes=64, offset=0)
-        dst_s = shared.tile([P, S], U8, name="dst_s", align_bytes=64, offset=S)
+        src_s = sb("src_s", [P, S], U8)
+        dst_s = sb("dst_s", [P, S], U8)
         src_w = sb("src_w", [P, S], U32)
         dst_w = sb("dst_w", [P, S], U32)
         nc.vector.tensor_copy(src_s[:], xs_tab[:].indirect(offs_t[:]))
         nc.vector.tensor_copy(dst_s[:], xs_tab[:].indirect(dst_t[:]))
-
-        w1_b = sb("w1_b", [P, PACK * H], BF16)
-        w1_q = sb("w1_q", [P, H], U32)
-        w1_s = sb("w1_s", [P, H], U8)
-        nc.scalar.copy(
-            out=w1_b[:].rearrange("p (t m j) -> p m j t", t=PACK, j=PACK),
-            in_=w1_raw[:].rearrange("p j (m t) -> p m j t", t=PACK),
-        )
         nc.vector.tensor_copy(src_w[:], xw_tab[:].indirect(offs_t[:]))
         nc.vector.tensor_copy(dst_w[:], xw_tab[:].indirect(dst_t[:]))
-        nc.vector.quantize_mx(out=w1_q[:].bitcast(FP8X4), scales=w1_s[:], in_=w1_b[:])
+
+        def deal(dealt, dealt_s, raw, raw_s):
+            nc.vector.tensor_copy(
+                out=dealt[:].bitcast(U16).rearrange("p (t m) -> p t m", t=PACK),
+                in_=raw[:].bitcast(U16).rearrange("p (m t) -> p t m", t=PACK),
+            )
+            nc.vector.tensor_copy(
+                out=dealt_s[:].rearrange("p (t m) -> p t m", t=PACK),
+                in_=raw_s[:].rearrange("p (m t) -> p t m", t=PACK),
+            )
+
+        w4_q = sb("w4_q", [P, 2 * N], U8)
+        w4_s = sb("w4_s", [P, N], U8)
+        deal(w4_q, w4_s, w4_raw, w4s_raw)
+        HM = P // 2
+        w1_b = sb("w1_b", [P, PACK * H], BF16)
+        w1_q = sb("w1_q", [P, H], U32)
+        w1_bv = w1_b[:].rearrange("p (t m j) -> p m j t", t=PACK, j=PACK)
+        w1_rv = w1_raw[:].rearrange("p j (m t) -> p m j t", t=PACK)
+        nc.scalar.copy(out=w1_bv, in_=w1_rv)
 
         v_ps = [psum.tile([P, PACK, CH], F32, name="v_ps%d" % c) for c in range(NCH)]
         for c in range(NCH):
@@ -109,36 +114,35 @@ def tile_picked_zgatt_exp_po_kernel(
                 nc.tensor.matmul_mx(
                     out=v_ps[c][:, t, :],
                     lhsT=w4_q[:, 2 * P * t : 2 * P * (t + 1)].bitcast(FP4X4),
-                    lhsT_scale=ws_q[:, P * t : P * (t + 1)],
+                    lhsT_scale=w4_s[:, P * t : P * (t + 1)],
                     rhs=src_w[:, cols].bitcast(FP8X4),
                     rhs_scale=src_s[:, cols],
                     start=True,
                     stop=True,
                 )
 
-        w2_b = sb("w2_b", [P, PACK * H], BF16)
+        w2_b = at("w2_b", [P, PACK * H], BF16, 0)
         w2_q = sb("w2_q", [P, H], U32)
         w2_s = sb("w2_s", [P, H], U8)
-        HM = P // 2
         w2_bv = w2_b[:].rearrange("p (t m j) -> p m j t", t=PACK, j=PACK)
-
-        def quant_w2(h, t):
-            c0 = P * t + HM * h
-            nc.vector.quantize_mx(
-                out=w2_q[:, c0 : c0 + HM].bitcast(FP8X4),
-                scales=w2_s[:, c0 : c0 + HM],
-                in_=w2_b[:, PACK * c0 : PACK * (c0 + HM)],
-            )
-
-        raw0 = w2_raw[0][:].rearrange("p j (m t) -> p m j t", t=PACK)
-        raw1 = w2_raw[1][:].rearrange("p j (m t) -> p m j t", t=PACK)
-        nc.scalar.copy(out=w2_bv[:, 0:HM], in_=raw0)
-        for t in range(PACK):
-            quant_w2(0, t)
-        nc.vector.tensor_copy(out=w2_bv[:, HM:P, :, 0:2], in_=raw1[:, :, :, 0:2])
-        nc.scalar.copy(out=w2_bv[:, HM:P, :, 2:4], in_=raw1[:, :, :, 2:4])
-        for t in range(PACK):
-            quant_w2(1, t)
+        for h in range(2):
+            share = (HM, 16)[h]
+            if share < HM:
+                nc.scalar.copy(out=w2_bv[:, HM * h + share : HM * (h + 1)], in_=w2_raw[h][:, share:HM])
+            nc.vector.tensor_copy(out=w2_bv[:, HM * h : HM * h + share], in_=w2_raw[h][:, 0:share])
+            if h == 0:
+                w1_s = sb("w1_s", [P, H], U8, tag="w2_raw0")
+                nc.vector.quantize_mx(out=w1_q[:].bitcast(FP8X4), scales=w1_s[:], in_=w1_b[:])
+            for t in range(PACK):
+                c0 = P * t + HM * h
+                nc.vector.quantize_mx(
+                    out=w2_q[:, c0 : c0 + HM].bitcast(FP8X4),
+                    scales=w2_s[:, c0 : c0 + HM],
+                    in_=w2_b[:, PACK * c0 : PACK * (c0 + HM)],
+                )
+        w3_q = at("w3_q", [P, 2 * N], U8, 0)
+        w3_s = at("w3_s", [P, N], U8, 1024)
+        deal(w3_q, w3_s, w3_raw, w3s_raw)
 
         y_ps = [psum.tile([P, PACK, CH], F32, name="y_ps%d" % c) for c in range(NCH)]
         small = [sb("small%d" % c, [P, CH * PACK], F32) for c in range(NCH)]
@@ -184,15 +188,15 @@ def tile_picked_zgatt_exp_po_kernel(
                 nc.tensor.matmul_mx(
                     out=y_ps[c][:, t, :],
                     lhsT=w3_q[:, 2 * P * t : 2 * P * (t + 1)].bitcast(FP4X4),
-                    lhsT_scale=ws_q[:, N + P * t : N + P * (t + 1)],
+                    lhsT_scale=w3_s[:, P * t : P * (t + 1)],
                     rhs=h_q[c][:].bitcast(FP8X4),
                     rhs_scale=h_s[c][:],
                     start=True,
                     stop=True,
                 )
-            nc.scalar.activation(out=e_f[c][:], in_=y_ps[c][:], func=ACT.Exp)
 
         def message(c):
+            nc.scalar.activation(out=e_f[c][:], in_=y_ps[c][:], func=ACT.Exp)
             nc.vector.tensor_tensor(out=o_f[c][:], in0=v_ps[c][:], in1=e_f[c][:], op=ALU.mult)
             nc.sync.dma_start(out=out_rows[:, :, c * CH : (c + 1) * CH], in_=o_f[c][:])
 
@@ -209,14 +213,20 @@ def tile_picked_zgatt_exp_po_kernel(
             nc.vector.quantize_mx(out=o_q[:, cols].bitcast(FP8X4), scales=o_s[:, cols], in_=o_b[c][:])
             nc.sync.dma_start(out=out_words[:, cols], in_=o_q[:, cols].bitcast(I32))
 
+        hidden_mm(0)
+        for c in range(NCH + 1):
+            if c + 1 < NCH:
+                hidden_mm(c + 1)
+            if c < NCH:
+                leaky(c)
+            if c >= 1:
+                scores(c - 1)
         for c in range(NCH):
-            hidden_mm(c)
-        stages = (leaky, scores, message, round_out, planes)
-        lag = (0, 1, 3, 4, 5)
-        for step in range(NCH + lag[-1]):
-            for stage, d in zip(stages, lag):
-                if 0 <= step - d < NCH:
-                    stage(step - d)
+            message(c)
+        for c in range(NCH):
+            round_out(c)
+        for c in range(NCH):
+            planes(c)
         for q in range(4):
             queue = nc.scalar if q % 2 else nc.sync
             queue.dma_start(

@@ -21,6 +21,8 @@ PACK = 4
 CH = 128
 NCH = S // CH
 SLOPE = 0.2
+W1_VECTOR = 48
+W2_VECTOR = (0, 42)
 
 
 def tile_picked_zgatt_exp_po_kernel(
@@ -39,7 +41,7 @@ def tile_picked_zgatt_exp_po_kernel(
             return shared.tile(shape, dtype, name=name, align_bytes=64, offset=offset)
 
         xs_tab = sb("xs_tab", [P, T], U8)
-        w4s_raw = at("w4s_raw", [P, N], U8, 0)
+        w4s_raw = sb("w4s_raw", [P, N], U8)
         w3s_raw = sb("w3s_raw", [P, N], U8)
         nc.vector.memset(xs_tab[:].bitcast(I32), 0)
         nc.vector.memset(w4s_raw[:].bitcast(I32), 0)
@@ -65,15 +67,15 @@ def tile_picked_zgatt_exp_po_kernel(
         dst_t = sb("dst_t", [P, S // 16], U16)
         nc.sync.dma_start(offs_t[:], offs)
         nc.sync.dma_start(dst_t[:], dst)
+        w4_raw = sb("w4_raw", [P, 2 * N], U8)
+        nc.sync.dma_start(out=w4_raw[:].bitcast(I32), in_=w4_words[0].bitcast(I32))
         load_scales(xs_tab, x_scales, nc.sync)
         xw_tab = sb("xw_tab", [P, T], U32)
         nc.sync.dma_start(out=xw_tab[:].bitcast(I32), in_=x_words[0].rearrange("p n t -> p (n t)").bitcast(I32))
+        w3_raw = sb("w3_raw", [P, 2 * N], U8)
+        load_scales(w4s_raw, w4_scales, nc.sync)
         w1_raw = sb("w1_raw", [P, PACK, H], F32)
         nc.sync.dma_start(out=w1_raw[:], in_=w1.rearrange("(p j) c -> p j c", j=PACK))
-        w4_raw = sb("w4_raw", [P, 2 * N], U8)
-        w3_raw = sb("w3_raw", [P, 2 * N], U8)
-        nc.sync.dma_start(out=w4_raw[:].bitcast(I32), in_=w4_words[0].bitcast(I32))
-        load_scales(w4s_raw, w4_scales, nc.sync)
         w2_raw = [load_half("w2_raw%d" % h, w2, h) for h in range(2)]
         nc.sync.dma_start(out=w3_raw[:].bitcast(I32), in_=w3_words[0].bitcast(I32))
         load_scales(w3s_raw, w3_scales, nc.sync)
@@ -105,7 +107,10 @@ def tile_picked_zgatt_exp_po_kernel(
         w1_q = sb("w1_q", [P, H], U32)
         w1_bv = w1_b[:].rearrange("p (t m j) -> p m j t", t=PACK, j=PACK)
         w1_rv = w1_raw[:].rearrange("p j (m t) -> p m j t", t=PACK)
-        nc.scalar.copy(out=w1_bv, in_=w1_rv)
+        w1_s = sb("w1_s", [P, H], U8)
+        nc.scalar.copy(out=w1_bv[:, W1_VECTOR:], in_=w1_rv[:, W1_VECTOR:])
+        nc.vector.tensor_copy(out=w1_bv[:, :W1_VECTOR], in_=w1_rv[:, :W1_VECTOR])
+        nc.vector.quantize_mx(out=w1_q[:].bitcast(FP8X4), scales=w1_s[:], in_=w1_b[:])
 
         v_ps = [psum.tile([P, PACK, CH], F32, name="v_ps%d" % c) for c in range(NCH)]
         for c in range(NCH):
@@ -122,24 +127,18 @@ def tile_picked_zgatt_exp_po_kernel(
                 )
 
         w2_b = at("w2_b", [P, PACK * H], BF16, 0)
-        w2_q = sb("w2_q", [P, H], U32)
-        w2_s = sb("w2_s", [P, H], U8)
+        w2_q = [sb("w2_q%d" % t, [P, P], U32) for t in range(PACK)]
+        w2_s = [sb("w2_s%d" % t, [P, P], U8) for t in range(PACK)]
         w2_bv = w2_b[:].rearrange("p (t m j) -> p m j t", t=PACK, j=PACK)
         for h in range(2):
-            share = (HM, 16)[h]
-            if share < HM:
-                nc.scalar.copy(out=w2_bv[:, HM * h + share : HM * (h + 1)], in_=w2_raw[h][:, share:HM])
-            nc.vector.tensor_copy(out=w2_bv[:, HM * h : HM * h + share], in_=w2_raw[h][:, 0:share])
-            if h == 0:
-                w1_s = sb("w1_s", [P, H], U8, tag="w2_raw0")
-                nc.vector.quantize_mx(out=w1_q[:].bitcast(FP8X4), scales=w1_s[:], in_=w1_b[:])
-            for t in range(PACK):
-                c0 = P * t + HM * h
-                nc.vector.quantize_mx(
-                    out=w2_q[:, c0 : c0 + HM].bitcast(FP8X4),
-                    scales=w2_s[:, c0 : c0 + HM],
-                    in_=w2_b[:, PACK * c0 : PACK * (c0 + HM)],
-                )
+            share = W2_VECTOR[h]
+            nc.scalar.copy(out=w2_bv[:, HM * h + share : HM * (h + 1)], in_=w2_raw[h][:, share:HM])
+            if share:
+                nc.vector.tensor_copy(out=w2_bv[:, HM * h : HM * h + share], in_=w2_raw[h][:, 0:share])
+        for t in range(PACK):
+            nc.vector.quantize_mx(
+                out=w2_q[t][:].bitcast(FP8X4), scales=w2_s[t][:], in_=w2_b[:, PACK * P * t : PACK * P * (t + 1)]
+            )
         w3_q = at("w3_q", [P, 2 * N], U8, 0)
         w3_s = at("w3_s", [P, N], U8, 1024)
         deal(w3_q, w3_s, w3_raw, w3s_raw)
@@ -159,14 +158,14 @@ def tile_picked_zgatt_exp_po_kernel(
 
         def hidden_mm(c):
             cols = slice(c * CH, (c + 1) * CH)
-            for t in range(PACK):
+            for t in (range(PACK) if c == 0 else reversed(range(PACK))):
                 m = slice(P * t, P * (t + 1))
                 nc.tensor.matmul_mx(
                     out=y_ps[c][:, t, :], lhsT=w1_q[:, m].bitcast(FP8X4), lhsT_scale=w1_s[:, m],
                     rhs=src_w[:, cols].bitcast(FP8X4), rhs_scale=src_s[:, cols], start=True, stop=False,
                 )
                 nc.tensor.matmul_mx(
-                    out=y_ps[c][:, t, :], lhsT=w2_q[:, m].bitcast(FP8X4), lhsT_scale=w2_s[:, m],
+                    out=y_ps[c][:, t, :], lhsT=w2_q[t][:].bitcast(FP8X4), lhsT_scale=w2_s[t][:],
                     rhs=dst_w[:, cols].bitcast(FP8X4), rhs_scale=dst_s[:, cols], start=False, stop=True,
                 )
 
@@ -182,11 +181,16 @@ def tile_picked_zgatt_exp_po_kernel(
                 op=ALU.max,
             )
 
+        def score_bank(c, t):
+            return y_ps[0] if c == NCH - 1 and t >= PACK // 2 else y_ps[c]
+
         def scores(c):
             nc.vector.quantize_mx(out=h_q[c][:].bitcast(FP8X4), scales=h_s[c][:], in_=h_b[c][:])
+            if c == NCH - 1:
+                nc.scalar.activation(out=e_f[0][:], in_=y_ps[0][:], func=ACT.Exp)
             for t in range(PACK):
                 nc.tensor.matmul_mx(
-                    out=y_ps[c][:, t, :],
+                    out=score_bank(c, t)[:, t, :],
                     lhsT=w3_q[:, 2 * P * t : 2 * P * (t + 1)].bitcast(FP4X4),
                     lhsT_scale=w3_s[:, P * t : P * (t + 1)],
                     rhs=h_q[c][:].bitcast(FP8X4),
@@ -196,8 +200,12 @@ def tile_picked_zgatt_exp_po_kernel(
                 )
 
         def message(c):
-            nc.scalar.activation(out=e_f[c][:], in_=y_ps[c][:], func=ACT.Exp)
-            nc.vector.tensor_tensor(out=o_f[c][:], in0=v_ps[c][:], in1=e_f[c][:], op=ALU.mult)
+            step = PACK // 2 if c == NCH - 1 else PACK
+            for t in range(0, PACK, step):
+                rows = slice(t, t + step)
+                if c > 0:
+                    nc.scalar.activation(out=e_f[c][:, rows], in_=score_bank(c, t)[:, rows], func=ACT.Exp)
+                nc.vector.tensor_tensor(out=o_f[c][:, rows], in0=v_ps[c][:, rows], in1=e_f[c][:, rows], op=ALU.mult)
             nc.sync.dma_start(out=out_rows[:, :, c * CH : (c + 1) * CH], in_=o_f[c][:])
 
         def round_out(c):
@@ -211,7 +219,9 @@ def tile_picked_zgatt_exp_po_kernel(
         def planes(c):
             cols = slice(c * CH, (c + 1) * CH)
             nc.vector.quantize_mx(out=o_q[:, cols].bitcast(FP8X4), scales=o_s[:, cols], in_=o_b[c][:])
-            nc.sync.dma_start(out=out_words[:, cols], in_=o_q[:, cols].bitcast(I32))
+            if c >= NCH - 2:
+                done = cols if c == NCH - 1 else slice(0, (c + 1) * CH)
+                nc.sync.dma_start(out=out_words[:, done], in_=o_q[:, done].bitcast(I32))
 
         hidden_mm(0)
         for c in range(NCH + 1):

@@ -21,8 +21,8 @@ PACK = 4
 CH = 128
 NCH = S // CH
 SLOPE = 0.2
-W1_VECTOR = 48
-W2_VECTOR = (0, 42)
+W1_VECTOR = 52
+W2_VECTOR = (22, 38)
 
 
 def tile_picked_zgatt_exp_po_kernel(
@@ -46,10 +46,6 @@ def tile_picked_zgatt_exp_po_kernel(
         nc.vector.memset(xs_tab[:].bitcast(I32), 0)
         nc.vector.memset(w4s_raw[:].bitcast(I32), 0)
         nc.vector.memset(w3s_raw[:].bitcast(I32), 0)
-        warm_in = sb("warm_in", [P, 1], F32)
-        warm_out = sb("warm_out", [P, 1], F32)
-        nc.vector.memset(warm_in[:], 0.0)
-        nc.scalar.activation(out=warm_out[:], in_=warm_in[:], func=ACT.Exp)
 
         def load_scales(tile, rows, queue):
             for q in range(4):
@@ -150,7 +146,10 @@ def tile_picked_zgatt_exp_po_kernel(
         h_s = [sb("h_s%d" % c, [P, CH], U8) for c in range(NCH)]
         e_f = [sb("e_f%d" % c, [P, PACK, CH], F32) for c in range(NCH)]
         o_f = [sb("o_f%d" % c, [P, PACK, CH], F32) for c in range(NCH)]
-        o_b = [sb("o_b%d" % c, [P, CH * PACK], BF16) for c in range(NCH)]
+        o_b01 = sb("o_b01", [P, 2 * CH * PACK], BF16)
+        o_b = [o_b01[:, : CH * PACK], o_b01[:, CH * PACK :]] + [
+            sb("o_b%d" % c, [P, CH * PACK], BF16)[:] for c in range(2, NCH)
+        ]
         o_q = sb("o_q", [P, S], U32)
         o_s = sb("o_s", [P, S], U8)
         out_rows = out_0.rearrange("(p t) n -> p t n", t=PACK)
@@ -209,16 +208,29 @@ def tile_picked_zgatt_exp_po_kernel(
             nc.sync.dma_start(out=out_rows[:, :, c * CH : (c + 1) * CH], in_=o_f[c][:])
 
         def round_out(c):
-            dst_v = o_b[c][:].rearrange("p (n i t) -> p n t i", i=4, t=PACK)
+            dst_v = o_b[c].rearrange("p (n i t) -> p n t i", i=4, t=PACK)
             src_v = o_f[c][:].rearrange("p t (n i) -> p n t i", i=4)
-            if c == NCH - 1:
-                nc.vector.tensor_copy(out=dst_v, in_=src_v)
+            if c < 2:
+                nc.gpsimd.tensor_scalar(
+                    out=o_b[c].rearrange("p (n t) -> p n t", t=PACK),
+                    in0=o_f[c][:].rearrange("p t n -> p n t"),
+                    scalar1=1.0, scalar2=-0.0, op0=ALU.mult, op1=ALU.add,
+                )
+            elif c == NCH - 1:
+                nc.vector.tensor_copy(out=dst_v[:, :16], in_=src_v[:, :16])
+                nc.scalar.copy(out=dst_v[:, 16:], in_=src_v[:, 16:])
             else:
                 nc.scalar.copy(out=dst_v, in_=src_v)
 
         def planes(c):
             cols = slice(c * CH, (c + 1) * CH)
-            nc.vector.quantize_mx(out=o_q[:, cols].bitcast(FP8X4), scales=o_s[:, cols], in_=o_b[c][:])
+            if c == 0:
+                return
+            if c == 1:
+                both = slice(0, 2 * CH)
+                nc.vector.quantize_mx(out=o_q[:, both].bitcast(FP8X4), scales=o_s[:, both], in_=o_b01[:])
+            else:
+                nc.vector.quantize_mx(out=o_q[:, cols].bitcast(FP8X4), scales=o_s[:, cols], in_=o_b[c])
             if c >= NCH - 2:
                 done = cols if c == NCH - 1 else slice(0, (c + 1) * CH)
                 nc.sync.dma_start(out=out_words[:, done], in_=o_q[:, done].bitcast(I32))

@@ -57,7 +57,7 @@ def tile_picked_zgatt_exp_po_kernel(
             piece = sb(name, [P, PACK, H // 2], F32)
             view = w.rearrange("(p j) c -> p j c", j=PACK)
             nc.sync.dma_start(out=piece[:], in_=view[:, :, h * (H // 2) : (h + 1) * (H // 2)])
-            return piece[:].rearrange("p j (m t) -> p m j t", t=PACK)
+            return piece[:].rearrange("p j (m u t) -> p u m j t", u=2, t=2)
 
         offs_t = sb("offs_t", [P, S // 16], U16)
         dst_t = sb("dst_t", [P, S // 16], U16)
@@ -101,11 +101,11 @@ def tile_picked_zgatt_exp_po_kernel(
         HM = P // 2
         w1_b = sb("w1_b", [P, PACK * H], BF16)
         w1_q = sb("w1_q", [P, H], U32)
-        w1_bv = w1_b[:].rearrange("p (t m j) -> p m j t", t=PACK, j=PACK)
-        w1_rv = w1_raw[:].rearrange("p j (m t) -> p m j t", t=PACK)
+        w1_bv = w1_b[:].rearrange("p (u t m j) -> p u m j t", u=2, t=2, j=PACK)
+        w1_rv = w1_raw[:].rearrange("p j (m u t) -> p u m j t", u=2, t=2)
         w1_s = sb("w1_s", [P, H], U8)
-        nc.scalar.copy(out=w1_bv[:, W1_VECTOR:], in_=w1_rv[:, W1_VECTOR:])
-        nc.vector.tensor_copy(out=w1_bv[:, :W1_VECTOR], in_=w1_rv[:, :W1_VECTOR])
+        nc.scalar.copy(out=w1_bv[:, :, W1_VECTOR:], in_=w1_rv[:, :, W1_VECTOR:])
+        nc.vector.tensor_copy(out=w1_bv[:, :, :W1_VECTOR], in_=w1_rv[:, :, :W1_VECTOR])
         nc.vector.quantize_mx(out=w1_q[:].bitcast(FP8X4), scales=w1_s[:], in_=w1_b[:])
 
         v_ps = [psum.tile([P, PACK, CH], F32, name="v_ps%d" % c) for c in range(NCH)]
@@ -125,12 +125,12 @@ def tile_picked_zgatt_exp_po_kernel(
         w2_b = at("w2_b", [P, PACK * H], BF16, 0)
         w2_q = [sb("w2_q%d" % t, [P, P], U32) for t in range(PACK)]
         w2_s = [sb("w2_s%d" % t, [P, P], U8) for t in range(PACK)]
-        w2_bv = w2_b[:].rearrange("p (t m j) -> p m j t", t=PACK, j=PACK)
+        w2_bv = w2_b[:].rearrange("p (u t m j) -> p u m j t", u=2, t=2, j=PACK)
         for h in range(2):
             share = W2_VECTOR[h]
-            nc.scalar.copy(out=w2_bv[:, HM * h + share : HM * (h + 1)], in_=w2_raw[h][:, share:HM])
+            nc.scalar.copy(out=w2_bv[:, :, HM * h + share : HM * (h + 1)], in_=w2_raw[h][:, :, share:HM])
             if share:
-                nc.vector.tensor_copy(out=w2_bv[:, HM * h : HM * h + share], in_=w2_raw[h][:, 0:share])
+                nc.vector.tensor_copy(out=w2_bv[:, :, HM * h : HM * h + share], in_=w2_raw[h][:, :, 0:share])
         for t in range(PACK):
             nc.vector.quantize_mx(
                 out=w2_q[t][:].bitcast(FP8X4), scales=w2_s[t][:], in_=w2_b[:, PACK * P * t : PACK * P * (t + 1)]

@@ -145,7 +145,8 @@ def tile_picked_zgatt_exp_po_kernel(
         h_q = [sb("h_q%d" % c, [P, CH], U32) for c in range(NCH)]
         h_s = [sb("h_s%d" % c, [P, CH], U8) for c in range(NCH)]
         e_f = [sb("e_f%d" % c, [P, PACK, CH], F32) for c in range(NCH)]
-        o_f = [sb("o_f%d" % c, [P, PACK, CH], F32) for c in range(NCH)]
+        o_f23 = sb("o_f23", [P, PACK, 2 * CH], F32)
+        o_f = [sb("o_f%d" % c, [P, PACK, CH], F32)[:] for c in range(2)] + [o_f23[:, :, :CH], o_f23[:, :, CH:]]
         o_b01 = sb("o_b01", [P, 2 * CH * PACK], BF16)
         o_b = [o_b01[:, : CH * PACK], o_b01[:, CH * PACK :]] + [
             sb("o_b%d" % c, [P, CH * PACK], BF16)[:] for c in range(2, NCH)
@@ -205,15 +206,18 @@ def tile_picked_zgatt_exp_po_kernel(
                 if c > 0:
                     nc.scalar.activation(out=e_f[c][:, rows], in_=score_bank(c, t)[:, rows], func=ACT.Exp)
                 nc.vector.tensor_tensor(out=o_f[c][:, rows], in0=v_ps[c][:, rows], in1=e_f[c][:, rows], op=ALU.mult)
-            nc.sync.dma_start(out=out_rows[:, :, c * CH : (c + 1) * CH], in_=o_f[c][:])
+                if c == NCH - 1:
+                    nc.sync.dma_start(out=out_rows[:, rows, 2 * CH :], in_=o_f23[:, rows])
+            if c < 2:
+                nc.sync.dma_start(out=out_rows[:, :, c * CH : (c + 1) * CH], in_=o_f[c])
 
         def round_out(c):
             dst_v = o_b[c].rearrange("p (n i t) -> p n t i", i=4, t=PACK)
-            src_v = o_f[c][:].rearrange("p t (n i) -> p n t i", i=4)
+            src_v = o_f[c].rearrange("p t (n i) -> p n t i", i=4)
             if c < 2:
                 nc.gpsimd.tensor_scalar(
                     out=o_b[c].rearrange("p (n t) -> p n t", t=PACK),
-                    in0=o_f[c][:].rearrange("p t n -> p n t"),
+                    in0=o_f[c].rearrange("p t n -> p n t"),
                     scalar1=1.0, scalar2=-0.0, op0=ALU.mult, op1=ALU.add,
                 )
             elif c == NCH - 1:

@@ -21,8 +21,9 @@ PACK = 4
 CH = 128
 NCH = S // CH
 SLOPE = 0.2
-W1_VECTOR = 52
-W2_VECTOR = (22, 38)
+W1_VECTOR = 64
+W2_CUTS = (0, 96, 128)
+W2_VECTOR = (52, 20)
 
 
 def tile_picked_zgatt_exp_po_kernel(
@@ -48,23 +49,22 @@ def tile_picked_zgatt_exp_po_kernel(
         nc.vector.memset(w3s_raw[:].bitcast(I32), 0)
 
         def load_scales(tile, rows, queue):
-            for q in range(4):
-                queue.dma_start(
-                    out=tile[32 * q : 32 * q + 4, :].bitcast(I32), in_=rows[0, 4 * q : 4 * q + 4, :].bitcast(I32)
-                )
+            for r in range(4):
+                queue.dma_start(out=tile[r:P:32, :].bitcast(I32), in_=rows[0, r:16:4, :].bitcast(I32))
 
         def load_half(name, w, h):
-            piece = sb(name, [P, PACK, H // 2], F32)
+            lo, hi = W2_CUTS[h], W2_CUTS[h + 1]
+            piece = sb(name, [P, PACK, PACK * (hi - lo)], F32)
             view = w.rearrange("(p j) c -> p j c", j=PACK)
-            nc.sync.dma_start(out=piece[:], in_=view[:, :, h * (H // 2) : (h + 1) * (H // 2)])
+            nc.sync.dma_start(out=piece[:], in_=view[:, :, PACK * lo : PACK * hi])
             return piece[:].rearrange("p j (m u t) -> p u m j t", u=2, t=2)
 
+        w4_raw = sb("w4_raw", [P, 2 * N], U8)
+        nc.sync.dma_start(out=w4_raw[:].bitcast(I32), in_=w4_words[0].bitcast(I32))
         offs_t = sb("offs_t", [P, S // 16], U16)
         dst_t = sb("dst_t", [P, S // 16], U16)
         nc.sync.dma_start(offs_t[:], offs)
         nc.sync.dma_start(dst_t[:], dst)
-        w4_raw = sb("w4_raw", [P, 2 * N], U8)
-        nc.sync.dma_start(out=w4_raw[:].bitcast(I32), in_=w4_words[0].bitcast(I32))
         load_scales(xs_tab, x_scales, nc.sync)
         xw_tab = sb("xw_tab", [P, T], U32)
         nc.sync.dma_start(out=xw_tab[:].bitcast(I32), in_=x_words[0].rearrange("p n t -> p (n t)").bitcast(I32))
@@ -79,11 +79,11 @@ def tile_picked_zgatt_exp_po_kernel(
         src_s = sb("src_s", [P, S], U8)
         dst_s = sb("dst_s", [P, S], U8)
         src_w = sb("src_w", [P, S], U32)
-        dst_w = sb("dst_w", [P, S], U32)
+        dst_w0 = sb("dst_w0", [P, S // 2], U32)
         nc.vector.tensor_copy(src_s[:], xs_tab[:].indirect(offs_t[:]))
         nc.vector.tensor_copy(dst_s[:], xs_tab[:].indirect(dst_t[:]))
         nc.vector.tensor_copy(src_w[:], xw_tab[:].indirect(offs_t[:]))
-        nc.vector.tensor_copy(dst_w[:], xw_tab[:].indirect(dst_t[:]))
+        nc.vector.tensor_copy(dst_w0[:], xw_tab[:].indirect(dst_t[:, : S // 32]))
 
         def deal(dealt, dealt_s, raw, raw_s):
             nc.vector.tensor_copy(
@@ -128,13 +128,17 @@ def tile_picked_zgatt_exp_po_kernel(
         w2_bv = w2_b[:].rearrange("p (u t m j) -> p u m j t", u=2, t=2, j=PACK)
         for h in range(2):
             share = W2_VECTOR[h]
-            nc.scalar.copy(out=w2_bv[:, :, HM * h + share : HM * (h + 1)], in_=w2_raw[h][:, :, share:HM])
+            lo, hi = W2_CUTS[h], W2_CUTS[h + 1]
+            nc.scalar.copy(out=w2_bv[:, :, lo + share : hi], in_=w2_raw[h][:, :, share:])
             if share:
-                nc.vector.tensor_copy(out=w2_bv[:, :, HM * h : HM * h + share], in_=w2_raw[h][:, :, 0:share])
+                nc.vector.tensor_copy(out=w2_bv[:, :, lo : lo + share], in_=w2_raw[h][:, :, 0:share])
         for t in range(PACK):
             nc.vector.quantize_mx(
                 out=w2_q[t][:].bitcast(FP8X4), scales=w2_s[t][:], in_=w2_b[:, PACK * P * t : PACK * P * (t + 1)]
             )
+        dst_w1 = at("dst_w1", [P, S // 2], U32, 2048)
+        nc.vector.tensor_copy(dst_w1[:], xw_tab[:].indirect(dst_t[:, S // 32 :]))
+        dst_w = [(dst_w0, dst_w1)[c // 2][:, (c % 2) * CH : (c % 2 + 1) * CH] for c in range(NCH)]
         w3_q = at("w3_q", [P, 2 * N], U8, 0)
         w3_s = at("w3_s", [P, N], U8, 1024)
         deal(w3_q, w3_s, w3_raw, w3s_raw)
@@ -166,7 +170,7 @@ def tile_picked_zgatt_exp_po_kernel(
                 )
                 nc.tensor.matmul_mx(
                     out=y_ps[c][:, t, :], lhsT=w2_q[t][:].bitcast(FP8X4), lhsT_scale=w2_s[t][:],
-                    rhs=dst_w[:, cols].bitcast(FP8X4), rhs_scale=dst_s[:, cols], start=False, stop=True,
+                    rhs=dst_w[c].bitcast(FP8X4), rhs_scale=dst_s[:, cols], start=False, stop=True,
                 )
 
         def leaky(c):
@@ -253,8 +257,6 @@ def tile_picked_zgatt_exp_po_kernel(
             round_out(c)
         for c in range(NCH):
             planes(c)
-        for q in range(4):
-            queue = nc.scalar if q % 2 else nc.sync
-            queue.dma_start(
-                out=out_2[0, 4 * q : 4 * q + 4, :].bitcast(I32), in_=o_s[32 * q : 32 * q + 4, :].bitcast(I32)
-            )
+        for r in range(4):
+            queue = nc.scalar if r % 2 else nc.sync
+            queue.dma_start(out=out_2[0, r:16:4, :].bitcast(I32), in_=o_s[r:P:32, :].bitcast(I32))

@@ -239,8 +239,8 @@ def tile_picked_zgatt_exp_po_kernel(
                 nc.vector.quantize_mx(out=o_q[:, both].bitcast(FP8X4), scales=o_s[:, both], in_=o_b01[:])
             else:
                 nc.vector.quantize_mx(out=o_q[:, cols].bitcast(FP8X4), scales=o_s[:, cols], in_=o_b[c])
-            if c >= NCH - 2:
-                done = cols if c == NCH - 1 else slice(0, (c + 1) * CH)
+            if c % 2:
+                done = slice((c - 1) * CH, (c + 1) * CH)
                 nc.sync.dma_start(out=out_words[:, done], in_=o_q[:, done].bitcast(I32))
 
         hidden_mm(0)

@@ -21,6 +21,8 @@ PACK = 4
 CH = 128
 NCH = S // CH
 SLOPE = 0.2
+EARLY = 2
+LIVE = P - 16
 W1_VECTOR = 64
 W2_CUTS = (0, 96, 128)
 W2_VECTOR = (52, 20)
@@ -41,12 +43,12 @@ def tile_picked_zgatt_exp_po_kernel(
         def at(name, shape, dtype, offset):
             return shared.tile(shape, dtype, name=name, align_bytes=64, offset=offset)
 
-        xs_tab = sb("xs_tab", [P, T], U8)
-        w4s_raw = sb("w4s_raw", [P, N], U8)
-        w3s_raw = sb("w3s_raw", [P, N], U8)
-        nc.vector.memset(xs_tab[:].bitcast(I32), 0)
-        nc.vector.memset(w4s_raw[:].bitcast(I32), 0)
-        nc.vector.memset(w3s_raw[:].bitcast(I32), 0)
+        xs_tab = at("xs_tab", [P, T], U8, 13312)
+        ws_raw = sb("ws_raw", [P, N], U8)
+        x_s = sb("x_s", [P, 2 * S], U8)
+        nc.vector.memset(ws_raw[:].bitcast(I32), 0)
+        nc.vector.memset(xs_tab[:LIVE, :].bitcast(I32), 0)
+        nc.vector.memset(x_s[:].bitcast(I32), 0)
 
         def load_scales(tile, rows, queue):
             for r in range(4):
@@ -54,50 +56,55 @@ def tile_picked_zgatt_exp_po_kernel(
 
         def load_half(name, w, h):
             lo, hi = W2_CUTS[h], W2_CUTS[h + 1]
-            piece = sb(name, [P, PACK, PACK * (hi - lo)], F32)
+            piece = at(name, [P, PACK, PACK * (hi - lo)], F32, (8192, 14336)[h])
             view = w.rearrange("(p j) c -> p j c", j=PACK)
             nc.sync.dma_start(out=piece[:], in_=view[:, :, PACK * lo : PACK * hi])
             return piece[:].rearrange("p j (m u t) -> p u m j t", u=2, t=2)
 
-        w4_raw = sb("w4_raw", [P, 2 * N], U8)
-        nc.sync.dma_start(out=w4_raw[:].bitcast(I32), in_=w4_words[0].bitcast(I32))
+        nc.sync.dma_start(out=xs_tab[LIVE:, :].bitcast(I32), in_=x_scales[0].bitcast(I32))
         offs_t = sb("offs_t", [P, S // 16], U16)
         dst_t = sb("dst_t", [P, S // 16], U16)
         nc.sync.dma_start(offs_t[:], offs)
         nc.sync.dma_start(dst_t[:], dst)
-        load_scales(xs_tab, x_scales, nc.sync)
+        w_raw = sb("w_raw", [P, 2 * N], U8)
+        nc.sync.dma_start(out=w_raw[:].bitcast(I32), in_=w4_words[0].bitcast(I32))
         xw_tab = sb("xw_tab", [P, T], U32)
         nc.sync.dma_start(out=xw_tab[:].bitcast(I32), in_=x_words[0].rearrange("p n t -> p (n t)").bitcast(I32))
-        w3_raw = sb("w3_raw", [P, 2 * N], U8)
-        load_scales(w4s_raw, w4_scales, nc.sync)
+        load_scales(ws_raw, w4_scales, nc.sync)
         w1_raw = sb("w1_raw", [P, PACK, H], F32)
         nc.sync.dma_start(out=w1_raw[:], in_=w1.rearrange("(p j) c -> p j c", j=PACK))
-        w2_raw = [load_half("w2_raw%d" % h, w2, h) for h in range(2)]
-        nc.sync.dma_start(out=w3_raw[:].bitcast(I32), in_=w3_words[0].bitcast(I32))
-        load_scales(w3s_raw, w3_scales, nc.sync)
 
-        src_s = sb("src_s", [P, S], U8)
-        dst_s = sb("dst_s", [P, S], U8)
-        src_w = sb("src_w", [P, S], U32)
-        dst_w0 = sb("dst_w0", [P, S // 2], U32)
-        nc.vector.tensor_copy(src_s[:], xs_tab[:].indirect(offs_t[:]))
-        nc.vector.tensor_copy(dst_s[:], xs_tab[:].indirect(dst_t[:]))
-        nc.vector.tensor_copy(src_w[:], xw_tab[:].indirect(offs_t[:]))
-        nc.vector.tensor_copy(dst_w0[:], xw_tab[:].indirect(dst_t[:, : S // 32]))
-
-        def deal(dealt, dealt_s, raw, raw_s):
+        def deal_words(dealt, raw):
             nc.vector.tensor_copy(
                 out=dealt[:].bitcast(U16).rearrange("p (t m) -> p t m", t=PACK),
                 in_=raw[:].bitcast(U16).rearrange("p (m t) -> p t m", t=PACK),
             )
+
+        def deal_scales(dealt, raw):
             nc.vector.tensor_copy(
-                out=dealt_s[:].rearrange("p (t m) -> p t m", t=PACK),
-                in_=raw_s[:].rearrange("p (m t) -> p t m", t=PACK),
+                out=dealt[:].rearrange("p (t m) -> p t m", t=PACK),
+                in_=raw[:].rearrange("p (m t) -> p t m", t=PACK),
             )
 
+        picked_s = at("picked_s", [P, 2 * S], U8, 4096)
+        src_s = x_s[:, :S]
+        dst_s = x_s[:, S:]
+        src_w = sb("src_w", [P, S], U32)
+        dst_w0 = sb("dst_w0", [P, S // 2], U32)
+        nc.vector.tensor_copy(picked_s[:, :S], xs_tab[:].indirect(offs_t[:]))
+        nc.vector.tensor_copy(picked_s[:, S:], xs_tab[:].indirect(dst_t[:]))
+        for r in range(4):
+            nc.sync.dma_start(out=x_s[r:P:32, :].bitcast(I32), in_=picked_s[LIVE + r : P : 4, :].bitcast(I32))
+        w2_raw = [load_half("w2_raw%d" % h, w2, h) for h in range(2)]
         w4_q = sb("w4_q", [P, 2 * N], U8)
+        deal_words(w4_q, w_raw)
+        nc.vector.tensor_copy(src_w[:], xw_tab[:].indirect(offs_t[:]))
+        nc.vector.tensor_copy(dst_w0[:], xw_tab[:].indirect(dst_t[:, : S // 32]))
+
         w4_s = sb("w4_s", [P, N], U8)
-        deal(w4_q, w4_s, w4_raw, w4s_raw)
+        deal_scales(w4_s, ws_raw)
+        nc.sync.dma_start(out=w_raw[:].bitcast(I32), in_=w3_words[0].bitcast(I32))
+        load_scales(ws_raw, w3_scales, nc.sync)
         HM = P // 2
         w1_b = sb("w1_b", [P, PACK * H], BF16)
         w1_q = sb("w1_q", [P, H], U32)
@@ -141,7 +148,8 @@ def tile_picked_zgatt_exp_po_kernel(
         dst_w = [(dst_w0, dst_w1)[c // 2][:, (c % 2) * CH : (c % 2 + 1) * CH] for c in range(NCH)]
         w3_q = at("w3_q", [P, 2 * N], U8, 0)
         w3_s = at("w3_s", [P, N], U8, 1024)
-        deal(w3_q, w3_s, w3_raw, w3s_raw)
+        deal_words(w3_q, w_raw)
+        deal_scales(w3_s, ws_raw)
 
         y_ps = [psum.tile([P, PACK, CH], F32, name="y_ps%d" % c) for c in range(NCH)]
         small = [sb("small%d" % c, [P, CH * PACK], F32) for c in range(NCH)]
@@ -160,18 +168,31 @@ def tile_picked_zgatt_exp_po_kernel(
         out_rows = out_0.rearrange("(p t) n -> p t n", t=PACK)
         out_words = out_1[0].rearrange("p n t -> p (n t)").bitcast(I32)
 
-        def hidden_mm(c):
+        def src_pass(c, t, start):
             cols = slice(c * CH, (c + 1) * CH)
-            for t in (range(PACK) if c == 0 else reversed(range(PACK))):
-                m = slice(P * t, P * (t + 1))
-                nc.tensor.matmul_mx(
-                    out=y_ps[c][:, t, :], lhsT=w1_q[:, m].bitcast(FP8X4), lhsT_scale=w1_s[:, m],
-                    rhs=src_w[:, cols].bitcast(FP8X4), rhs_scale=src_s[:, cols], start=True, stop=False,
-                )
-                nc.tensor.matmul_mx(
-                    out=y_ps[c][:, t, :], lhsT=w2_q[t][:].bitcast(FP8X4), lhsT_scale=w2_s[t][:],
-                    rhs=dst_w[c].bitcast(FP8X4), rhs_scale=dst_s[:, cols], start=False, stop=True,
-                )
+            m = slice(P * t, P * (t + 1))
+            nc.tensor.matmul_mx(
+                out=y_ps[c][:, t, :], lhsT=w1_q[:, m].bitcast(FP8X4), lhsT_scale=w1_s[:, m],
+                rhs=src_w[:, cols].bitcast(FP8X4), rhs_scale=src_s[:, cols], start=start, stop=False,
+            )
+
+        def dst_pass(c, t, stop):
+            cols = slice(c * CH, (c + 1) * CH)
+            nc.tensor.matmul_mx(
+                out=y_ps[c][:, t, :], lhsT=w2_q[t][:].bitcast(FP8X4), lhsT_scale=w2_s[t][:],
+                rhs=dst_w[c].bitcast(FP8X4), rhs_scale=dst_s[:, cols], start=False, stop=stop,
+            )
+
+        def hidden_mm(c):
+            order = list(range(PACK) if c == 0 else reversed(range(PACK)))
+            for t in order:
+                if c >= EARLY:
+                    src_pass(c, t, True)
+                dst_pass(c, t, c >= EARLY or t == order[-1])
+
+        for c in range(EARLY):
+            for t in range(PACK):
+                src_pass(c, t, t == 0)
 
         def leaky(c):
             y_nt = y_ps[c][:].rearrange("p t n -> p n t")

@@ -23,9 +23,9 @@ NCH = S // CH
 SLOPE = 0.2
 EARLY = 2
 LIVE = P - 16
-W1_VECTOR = 64
+W1_VECTOR = 80
 W2_CUTS = (0, 96, 128)
-W2_VECTOR = (52, 20)
+W2_VECTOR = (66, 22)
 
 
 def tile_picked_zgatt_exp_po_kernel(

@@ -20,12 +20,16 @@ P = 128
 PACK = 4
 CH = 128
 NCH = S // CH
+HALF = S // 2
 SLOPE = 0.2
-EARLY = 2
-LIVE = P - 16
-W1_VECTOR = 80
+X_ROWS = P - 16
+W_ROWS = P - 32
+W1_VECTOR = 60
 W2_CUTS = (0, 96, 128)
-W2_VECTOR = (66, 22)
+W2_VECTOR = (62, 20)
+LAST_VECTOR = 16
+W2R_AT, W3_AT, W2A_AT, XS_AT, W4_AT, W2B_AT = 0, 4096, 5120, 11200, 11264, 13184
+W1R_AT = 15360
 
 
 def tile_picked_zgatt_exp_po_kernel(
@@ -37,247 +41,248 @@ def tile_picked_zgatt_exp_po_kernel(
         shared = ctx.enter_context(tc.tile_pool(name="shared", bufs=1))
         psum = ctx.enter_context(tc.psum_pool(name="psum", bufs=1))
 
-        def sb(name, shape, dtype, tag=None):
-            return keep.tile(shape, dtype, name=name, tag=tag or name, align_bytes=64)
+        def sb(name, shape, dtype):
+            return keep.tile(shape, dtype, name=name, align_bytes=64)
 
         def at(name, shape, dtype, offset):
             return shared.tile(shape, dtype, name=name, align_bytes=64, offset=offset)
 
-        xs_tab = at("xs_tab", [P, T], U8, 13312)
+        def mx(out, w, w_scale, x, x_scale, start, stop):
+            nc.tensor.matmul_mx(
+                out=out, lhsT=w, lhsT_scale=w_scale, rhs=x.bitcast(FP8X4), rhs_scale=x_scale, start=start, stop=stop
+            )
+
+        def quantize(words, scales, values):
+            nc.vector.quantize_mx(out=words.bitcast(FP8X4), scales=scales, in_=values)
+
+        xs_tab = at("xs_tab", [P, T], U8, XS_AT)
         ws_raw = sb("ws_raw", [P, N], U8)
         x_s = sb("x_s", [P, 2 * S], U8)
-        nc.vector.memset(ws_raw[:].bitcast(I32), 0)
-        nc.vector.memset(xs_tab[:LIVE, :].bitcast(I32), 0)
+        w_s = sb("w_s", [P, 2 * N], U8)
+        nc.vector.memset(xs_tab[:X_ROWS, :].bitcast(I32), 0)
+        nc.vector.memset(ws_raw[:W_ROWS, :].bitcast(I32), 0)
         nc.vector.memset(x_s[:].bitcast(I32), 0)
+        nc.vector.memset(w_s[:].bitcast(I32), 0)
 
-        def load_scales(tile, rows, queue):
-            for r in range(4):
-                queue.dma_start(out=tile[r:P:32, :].bitcast(I32), in_=rows[0, r:16:4, :].bitcast(I32))
-
-        def load_half(name, w, h):
-            lo, hi = W2_CUTS[h], W2_CUTS[h + 1]
-            piece = at(name, [P, PACK, PACK * (hi - lo)], F32, (8192, 14336)[h])
-            view = w.rearrange("(p j) c -> p j c", j=PACK)
-            nc.sync.dma_start(out=piece[:], in_=view[:, :, PACK * lo : PACK * hi])
-            return piece[:].rearrange("p j (m u t) -> p u m j t", u=2, t=2)
-
-        nc.sync.dma_start(out=xs_tab[LIVE:, :].bitcast(I32), in_=x_scales[0].bitcast(I32))
         offs_t = sb("offs_t", [P, S // 16], U16)
         dst_t = sb("dst_t", [P, S // 16], U16)
+        nc.sync.dma_start(out=xs_tab[X_ROWS:, :].bitcast(I32), in_=x_scales[0].bitcast(I32))
         nc.sync.dma_start(offs_t[:], offs)
         nc.sync.dma_start(dst_t[:], dst)
-        w_raw = sb("w_raw", [P, 2 * N], U8)
-        nc.sync.dma_start(out=w_raw[:].bitcast(I32), in_=w4_words[0].bitcast(I32))
-        xw_tab = sb("xw_tab", [P, T], U32)
-        nc.sync.dma_start(out=xw_tab[:].bitcast(I32), in_=x_words[0].rearrange("p n t -> p (n t)").bitcast(I32))
-        load_scales(ws_raw, w4_scales, nc.sync)
         w1_raw = sb("w1_raw", [P, PACK, H], F32)
         nc.sync.dma_start(out=w1_raw[:], in_=w1.rearrange("(p j) c -> p j c", j=PACK))
-
-        def deal_words(dealt, raw):
-            nc.vector.tensor_copy(
-                out=dealt[:].bitcast(U16).rearrange("p (t m) -> p t m", t=PACK),
-                in_=raw[:].bitcast(U16).rearrange("p (m t) -> p t m", t=PACK),
+        for w, rows in enumerate((w3_scales, w4_scales)):
+            nc.sync.dma_start(
+                out=ws_raw[W_ROWS + w : P : 2, :].bitcast(I32),
+                in_=rows[0].bitcast(I32).rearrange("(q r) c -> r q c", r=4),
             )
+        xw_tab = sb("xw_tab", [P, T], U32)
+        nc.sync.dma_start(out=xw_tab[:].bitcast(I32), in_=x_words[0].rearrange("p n t -> p (n t)").bitcast(I32))
 
-        def deal_scales(dealt, raw):
-            nc.vector.tensor_copy(
-                out=dealt[:].rearrange("p (t m) -> p t m", t=PACK),
-                in_=raw[:].rearrange("p (m t) -> p t m", t=PACK),
-            )
-
-        picked_s = at("picked_s", [P, 2 * S], U8, 4096)
-        src_s = x_s[:, :S]
-        dst_s = x_s[:, S:]
-        src_w = sb("src_w", [P, S], U32)
-        dst_w0 = sb("dst_w0", [P, S // 2], U32)
+        picked_s = at("picked_s", [P, 2 * S], U8, W3_AT)
         nc.vector.tensor_copy(picked_s[:, :S], xs_tab[:].indirect(offs_t[:]))
         nc.vector.tensor_copy(picked_s[:, S:], xs_tab[:].indirect(dst_t[:]))
         for r in range(4):
-            nc.sync.dma_start(out=x_s[r:P:32, :].bitcast(I32), in_=picked_s[LIVE + r : P : 4, :].bitcast(I32))
-        w2_raw = [load_half("w2_raw%d" % h, w2, h) for h in range(2)]
-        w4_q = sb("w4_q", [P, 2 * N], U8)
-        deal_words(w4_q, w_raw)
-        nc.vector.tensor_copy(src_w[:], xw_tab[:].indirect(offs_t[:]))
-        nc.vector.tensor_copy(dst_w0[:], xw_tab[:].indirect(dst_t[:, : S // 32]))
+            nc.sync.dma_start(out=x_s[r:P:32, :].bitcast(I32), in_=picked_s[X_ROWS + r : P : 4, :].bitcast(I32))
 
-        w4_s = sb("w4_s", [P, N], U8)
-        deal_scales(w4_s, ws_raw)
-        nc.sync.dma_start(out=w_raw[:].bitcast(I32), in_=w3_words[0].bitcast(I32))
-        load_scales(ws_raw, w3_scales, nc.sync)
-        HM = P // 2
-        w1_b = sb("w1_b", [P, PACK * H], BF16)
+        w2_rows = w2.rearrange("(p j) c -> p j c", j=PACK)
+        w2_raw = []
+        for h in range(2):
+            lo, hi = W2_CUTS[h], W2_CUTS[h + 1]
+            piece = at("w2_raw%d" % h, [P, PACK, PACK * (hi - lo)], F32, (W2A_AT, W2B_AT)[h])
+            nc.sync.dma_start(out=piece[:], in_=w2_rows[:, :, PACK * lo : PACK * hi])
+            w2_raw.append(piece)
+        w4_raw = at("w4_raw", [P, 2 * N], U8, W4_AT)
+        w3_raw = at("w3_raw", [P, 2 * N], U8, W3_AT)
+        nc.sync.dma_start(out=w4_raw[:].bitcast(I32), in_=w4_words[0].bitcast(I32))
+        nc.sync.dma_start(out=w3_raw[:].bitcast(I32), in_=w3_words[0].bitcast(I32))
+
+        def round_weight(rounded, raw, lo, cut, hi):
+            dealt = rounded[:].rearrange("p (u t m j) -> p u m j t", u=2, t=2, j=PACK)
+            rows = raw[:].rearrange("p j (m u t) -> p u m j t", u=2, t=2)
+            nc.scalar.copy(out=dealt[:, :, cut:hi], in_=rows[:, :, cut - lo :])
+            nc.vector.tensor_copy(out=dealt[:, :, lo:cut], in_=rows[:, :, : cut - lo])
+
+        w1_b = at("w1_b", [P, PACK * H], BF16, W1R_AT)
         w1_q = sb("w1_q", [P, H], U32)
-        w1_bv = w1_b[:].rearrange("p (u t m j) -> p u m j t", u=2, t=2, j=PACK)
-        w1_rv = w1_raw[:].rearrange("p j (m u t) -> p u m j t", u=2, t=2)
         w1_s = sb("w1_s", [P, H], U8)
-        nc.scalar.copy(out=w1_bv[:, :, W1_VECTOR:], in_=w1_rv[:, :, W1_VECTOR:])
-        nc.vector.tensor_copy(out=w1_bv[:, :, :W1_VECTOR], in_=w1_rv[:, :, :W1_VECTOR])
-        nc.vector.quantize_mx(out=w1_q[:].bitcast(FP8X4), scales=w1_s[:], in_=w1_b[:])
+        round_weight(w1_b, w1_raw, 0, W1_VECTOR, P)
+        quantize(w1_q[:], w1_s[:], w1_b[:])
 
-        v_ps = [psum.tile([P, PACK, CH], F32, name="v_ps%d" % c) for c in range(NCH)]
+        ws_dealt = sb("ws_dealt", [P, N], U8)
+        nc.vector.tensor_copy(
+            out=ws_dealt[:].rearrange("p (t m) -> p t m", t=PACK), in_=ws_raw[:].rearrange("p (m t) -> p t m", t=PACK)
+        )
+        for r in range(4):
+            rows = slice(W_ROWS + 8 * r, W_ROWS + 8 * (r + 1))
+            nc.sync.dma_start(out=w_s[r:P:32, :].bitcast(I32), in_=ws_dealt[rows, :].bitcast(I32))
+
+        src_w0 = at("src_w0", [P, HALF], U32, W1R_AT)
+        src_w1 = at("src_w1", [P, HALF], U32, W1R_AT + 1024)
+        dst_w0 = at("dst_w0", [P, HALF], U32, W1R_AT + 2048)
+        y_ps = [psum.tile([P, PACK, CH], F32, name="y_ps%d" % c) for c in range(NCH)]
+
+        def chunk(halves, c):
+            return halves[c // 2][:, (c % 2) * CH : (c % 2 + 1) * CH]
+
+        for h, picked in enumerate((src_w0, src_w1)):
+            nc.vector.tensor_copy(picked[:], xw_tab[:].indirect(offs_t[:, h * HALF // 16 : (h + 1) * HALF // 16]))
+        nc.vector.tensor_copy(dst_w0[:], xw_tab[:].indirect(dst_t[:, : HALF // 16]))
         for c in range(NCH):
-            cols = slice(c * CH, (c + 1) * CH)
             for t in range(PACK):
-                nc.tensor.matmul_mx(
-                    out=v_ps[c][:, t, :],
-                    lhsT=w4_q[:, 2 * P * t : 2 * P * (t + 1)].bitcast(FP4X4),
-                    lhsT_scale=w4_s[:, P * t : P * (t + 1)],
-                    rhs=src_w[:, cols].bitcast(FP8X4),
-                    rhs_scale=src_s[:, cols],
-                    start=True,
-                    stop=True,
-                )
+                m = slice(P * t, P * (t + 1))
+                mx(y_ps[c][:, t, :], w1_q[:, m].bitcast(FP8X4), w1_s[:, m], chunk((src_w0, src_w1), c),
+                   x_s[:, c * CH : (c + 1) * CH], t == 0, False)
 
-        w2_b = at("w2_b", [P, PACK * H], BF16, 0)
+        w2_b = at("w2_b", [P, PACK * H], BF16, W2R_AT)
         w2_q = [sb("w2_q%d" % t, [P, P], U32) for t in range(PACK)]
         w2_s = [sb("w2_s%d" % t, [P, P], U8) for t in range(PACK)]
-        w2_bv = w2_b[:].rearrange("p (u t m j) -> p u m j t", u=2, t=2, j=PACK)
         for h in range(2):
-            share = W2_VECTOR[h]
             lo, hi = W2_CUTS[h], W2_CUTS[h + 1]
-            nc.scalar.copy(out=w2_bv[:, :, lo + share : hi], in_=w2_raw[h][:, :, share:])
-            if share:
-                nc.vector.tensor_copy(out=w2_bv[:, :, lo : lo + share], in_=w2_raw[h][:, :, 0:share])
+            round_weight(w2_b, w2_raw[h], lo, lo + W2_VECTOR[h], hi)
         for t in range(PACK):
-            nc.vector.quantize_mx(
-                out=w2_q[t][:].bitcast(FP8X4), scales=w2_s[t][:], in_=w2_b[:, PACK * P * t : PACK * P * (t + 1)]
-            )
-        dst_w1 = at("dst_w1", [P, S // 2], U32, 2048)
-        nc.vector.tensor_copy(dst_w1[:], xw_tab[:].indirect(dst_t[:, S // 32 :]))
-        dst_w = [(dst_w0, dst_w1)[c // 2][:, (c % 2) * CH : (c % 2 + 1) * CH] for c in range(NCH)]
-        w3_q = at("w3_q", [P, 2 * N], U8, 0)
-        w3_s = at("w3_s", [P, N], U8, 1024)
-        deal_words(w3_q, w_raw)
-        deal_scales(w3_s, ws_raw)
+            quantize(w2_q[t][:], w2_s[t][:], w2_b[:, PACK * P * t : PACK * P * (t + 1)])
+        dst_w1 = at("dst_w1", [P, HALF], U32, W2R_AT)
+        nc.vector.tensor_copy(dst_w1[:], xw_tab[:].indirect(dst_t[:, HALF // 16 :]))
 
-        y_ps = [psum.tile([P, PACK, CH], F32, name="y_ps%d" % c) for c in range(NCH)]
+        def dealt_words(tile):
+            return tile[:].bitcast(U16).rearrange("p (t m) -> p t m", t=PACK)
+
+        def raw_words(tile):
+            return tile[:].bitcast(U16).rearrange("p (m t) -> p t m", t=PACK)
+
+        w4_q = at("w4_q", [P, 2 * N], U8, W2B_AT)
+        w3_q = at("w3_q", [P, 2 * N], U8, W2R_AT + 1024)
+        nc.scalar.copy(out=dealt_words(w4_q), in_=raw_words(w4_raw))
+        nc.vector.tensor_copy(out=dealt_words(w3_q), in_=raw_words(w3_raw))
+
+        def packed(words, first, t):
+            return words[:, 2 * P * t : 2 * P * (t + 1)].bitcast(FP4X4), w_s[:, first + P * t : first + P * (t + 1)]
+
         small = [sb("small%d" % c, [P, CH * PACK], F32) for c in range(NCH)]
-        h_b = [sb("h_b%d" % c, [P, CH * PACK], BF16) for c in range(NCH)]
-        h_q = [sb("h_q%d" % c, [P, CH], U32) for c in range(NCH)]
-        h_s = [sb("h_s%d" % c, [P, CH], U8) for c in range(NCH)]
-        e_f = [sb("e_f%d" % c, [P, PACK, CH], F32) for c in range(NCH)]
-        o_f23 = sb("o_f23", [P, PACK, 2 * CH], F32)
-        o_f = [sb("o_f%d" % c, [P, PACK, CH], F32)[:] for c in range(2)] + [o_f23[:, :, :CH], o_f23[:, :, CH:]]
-        o_b01 = sb("o_b01", [P, 2 * CH * PACK], BF16)
-        o_b = [o_b01[:, : CH * PACK], o_b01[:, CH * PACK :]] + [
-            sb("o_b%d" % c, [P, CH * PACK], BF16)[:] for c in range(2, NCH)
+        h_b01 = sb("h_b01", [P, HALF * PACK], BF16)
+        h_b = [h_b01[:, : CH * PACK], h_b01[:, CH * PACK :]] + [
+            sb("h_b%d" % c, [P, CH * PACK], BF16)[:] for c in range(2, NCH)
         ]
+        h_q01 = sb("h_q01", [P, HALF], U32)
+        h_s01 = sb("h_s01", [P, HALF], U8)
+        h_q = {c: sb("h_q%d" % c, [P, CH], U32) for c in range(2, NCH)}
+        h_s = {c: sb("h_s%d" % c, [P, CH], U8) for c in range(2, NCH)}
+        e_f = [sb("e_f%d" % c, [P, PACK * CH], F32) for c in range(NCH)]
+        o_f01 = sb("o_f01", [P, PACK, HALF], F32)
+        o_f23 = sb("o_f23", [P, PACK, HALF], F32)
+        o_b01 = sb("o_b01", [P, HALF * PACK], BF16)
+        o_b = {c: sb("o_b%d" % c, [P, CH * PACK], BF16) for c in range(2, NCH)}
         o_q = sb("o_q", [P, S], U32)
         o_s = sb("o_s", [P, S], U8)
+        v_pair = [psum.tile([P, 2, HALF], F32, name="v_pair%d" % u) for u in range(2)]
+        v_ps = {c: psum.tile([P, PACK, CH], F32, name="v_ps%d" % c) for c in range(2, NCH)}
         out_rows = out_0.rearrange("(p t) n -> p t n", t=PACK)
         out_words = out_1[0].rearrange("p n t -> p (n t)").bitcast(I32)
 
-        def src_pass(c, t, start):
-            cols = slice(c * CH, (c + 1) * CH)
-            m = slice(P * t, P * (t + 1))
-            nc.tensor.matmul_mx(
-                out=y_ps[c][:, t, :], lhsT=w1_q[:, m].bitcast(FP8X4), lhsT_scale=w1_s[:, m],
-                rhs=src_w[:, cols].bitcast(FP8X4), rhs_scale=src_s[:, cols], start=start, stop=False,
-            )
-
-        def dst_pass(c, t, stop):
-            cols = slice(c * CH, (c + 1) * CH)
-            nc.tensor.matmul_mx(
-                out=y_ps[c][:, t, :], lhsT=w2_q[t][:].bitcast(FP8X4), lhsT_scale=w2_s[t][:],
-                rhs=dst_w[c].bitcast(FP8X4), rhs_scale=dst_s[:, cols], start=False, stop=stop,
-            )
-
-        def hidden_mm(c):
+        def close_hidden(c):
             order = list(range(PACK) if c == 0 else reversed(range(PACK)))
             for t in order:
-                if c >= EARLY:
-                    src_pass(c, t, True)
-                dst_pass(c, t, c >= EARLY or t == order[-1])
-
-        for c in range(EARLY):
-            for t in range(PACK):
-                src_pass(c, t, t == 0)
+                mx(y_ps[c][:, t, :], w2_q[t][:].bitcast(FP8X4), w2_s[t][:], chunk((dst_w0, dst_w1), c),
+                   x_s[:, S + c * CH : S + (c + 1) * CH], False, t == order[-1])
 
         def leaky(c):
             y_nt = y_ps[c][:].rearrange("p t n -> p n t")
-            nc.scalar.activation(
-                out=small[c][:].rearrange("p (n t) -> p n t", t=PACK), in_=y_nt, func=ACT.Copy, scale=SLOPE
-            )
+            small_nt = small[c][:].rearrange("p (n t) -> p n t", t=PACK)
+            nc.scalar.activation(out=small_nt, in_=y_nt, func=ACT.Copy, scale=SLOPE)
             nc.vector.tensor_tensor(
-                out=h_b[c][:].rearrange("p (n t) -> p n t", t=PACK),
-                in0=y_nt,
-                in1=small[c][:].rearrange("p (n t) -> p n t", t=PACK),
-                op=ALU.max,
+                out=h_b[c].rearrange("p (n t) -> p n t", t=PACK), in0=y_nt, in1=small_nt, op=ALU.max
             )
+
+        def pair_bank(u):
+            return y_ps[u][:].rearrange("p (a b) n -> p a (b n)", a=2)
+
+        def pair_values(u):
+            for a in range(2):
+                mx(v_pair[u][:, a, :], *packed(w4_q, N, 2 * u + a), src_w0[:], x_s[:, :HALF], True, True)
+
+        def chunk_values(c):
+            for t in range(PACK):
+                mx(v_ps[c][:, t, :], *packed(w4_q, N, t), chunk((src_w0, src_w1), c),
+                   x_s[:, c * CH : (c + 1) * CH], True, True)
+
+        def pair_scores(u):
+            for a in range(2):
+                mx(pair_bank(u)[:, a, :], *packed(w3_q, 0, 2 * u + a), h_q01[:], h_s01[:], True, True)
+            nc.scalar.activation(
+                out=e_f[u][:].rearrange("p (a n) -> p a n", a=2), in_=pair_bank(u), func=ACT.Exp
+            )
+
+        def pair_message(u):
+            rows = slice(2 * u, 2 * u + 2)
+            nc.vector.tensor_tensor(
+                out=o_f01[:, rows], in0=v_pair[u][:], in1=e_f[u][:].rearrange("p (a n) -> p a n", a=2), op=ALU.mult
+            )
+            nc.sync.dma_start(out=out_rows[:, rows, :HALF], in_=o_f01[:, rows])
 
         def score_bank(c, t):
             return y_ps[0] if c == NCH - 1 and t >= PACK // 2 else y_ps[c]
 
-        def scores(c):
-            nc.vector.quantize_mx(out=h_q[c][:].bitcast(FP8X4), scales=h_s[c][:], in_=h_b[c][:])
-            if c == NCH - 1:
-                nc.scalar.activation(out=e_f[0][:], in_=y_ps[0][:], func=ACT.Exp)
+        def chunk_scores(c):
+            quantize(h_q[c][:], h_s[c][:], h_b[c])
             for t in range(PACK):
-                nc.tensor.matmul_mx(
-                    out=score_bank(c, t)[:, t, :],
-                    lhsT=w3_q[:, 2 * P * t : 2 * P * (t + 1)].bitcast(FP4X4),
-                    lhsT_scale=w3_s[:, P * t : P * (t + 1)],
-                    rhs=h_q[c][:].bitcast(FP8X4),
-                    rhs_scale=h_s[c][:],
-                    start=True,
-                    stop=True,
-                )
+                mx(score_bank(c, t)[:, t, :], *packed(w3_q, 0, t), h_q[c][:], h_s[c][:], True, True)
 
-        def message(c):
+        def chunk_message(c):
             step = PACK // 2 if c == NCH - 1 else PACK
+            cols = slice((c - 2) * CH, (c - 1) * CH)
+            e_tn = e_f[c][:].rearrange("p (t n) -> p t n", t=PACK)
             for t in range(0, PACK, step):
                 rows = slice(t, t + step)
-                if c > 0:
-                    nc.scalar.activation(out=e_f[c][:, rows], in_=score_bank(c, t)[:, rows], func=ACT.Exp)
-                nc.vector.tensor_tensor(out=o_f[c][:, rows], in0=v_ps[c][:, rows], in1=e_f[c][:, rows], op=ALU.mult)
-                if c == NCH - 1:
-                    nc.sync.dma_start(out=out_rows[:, rows, 2 * CH :], in_=o_f23[:, rows])
-            if c < 2:
-                nc.sync.dma_start(out=out_rows[:, :, c * CH : (c + 1) * CH], in_=o_f[c])
-
-        def round_out(c):
-            dst_v = o_b[c].rearrange("p (n i t) -> p n t i", i=4, t=PACK)
-            src_v = o_f[c].rearrange("p t (n i) -> p n t i", i=4)
-            if c < 2:
-                nc.gpsimd.tensor_scalar(
-                    out=o_b[c].rearrange("p (n t) -> p n t", t=PACK),
-                    in0=o_f[c].rearrange("p t n -> p n t"),
-                    scalar1=1.0, scalar2=-0.0, op0=ALU.mult, op1=ALU.add,
+                nc.scalar.activation(out=e_tn[:, rows], in_=score_bank(c, t)[:, rows], func=ACT.Exp)
+                nc.vector.tensor_tensor(
+                    out=o_f23[:, rows, cols], in0=v_ps[c][:, rows], in1=e_tn[:, rows], op=ALU.mult
                 )
-            elif c == NCH - 1:
-                nc.vector.tensor_copy(out=dst_v[:, :16], in_=src_v[:, :16])
-                nc.scalar.copy(out=dst_v[:, 16:], in_=src_v[:, 16:])
-            else:
-                nc.scalar.copy(out=dst_v, in_=src_v)
+                if c == NCH - 1:
+                    nc.sync.dma_start(out=out_rows[:, rows, HALF:], in_=o_f23[:, rows])
 
-        def planes(c):
+        def round_views(c):
+            cols = slice((c - 2) * CH, (c - 1) * CH)
+            return (
+                o_b[c][:].rearrange("p (n i t) -> p n t i", i=4, t=PACK),
+                o_f23[:, :, cols].rearrange("p t (n i) -> p n t i", i=4),
+            )
+
+        for c in range(NCH):
+            close_hidden(c)
+        for u in range(2):
+            pair_values(u)
+        leaky(0)
+        leaky(1)
+        quantize(h_q01[:], h_s01[:], h_b01[:])
+        leaky(2)
+        leaky(3)
+        chunk_values(2)
+        pair_scores(0)
+        pair_scores(1)
+        chunk_values(3)
+        chunk_scores(2)
+        pair_message(0)
+        chunk_scores(3)
+        pair_message(1)
+        nc.gpsimd.tensor_scalar(
+            out=o_b01[:].rearrange("p (n t) -> p n t", t=PACK),
+            in0=o_f01[:].rearrange("p t n -> p n t"),
+            scalar1=1.0, scalar2=-0.0, op0=ALU.mult, op1=ALU.add,
+        )
+        chunk_message(2)
+        chunk_message(3)
+        rounded, exact = round_views(2)
+        nc.scalar.copy(out=rounded, in_=exact)
+        rounded, exact = round_views(3)
+        nc.vector.tensor_copy(out=rounded[:, :LAST_VECTOR], in_=exact[:, :LAST_VECTOR])
+        nc.scalar.copy(out=rounded[:, LAST_VECTOR:], in_=exact[:, LAST_VECTOR:])
+        quantize(o_q[:, :HALF], o_s[:, :HALF], o_b01[:])
+        nc.sync.dma_start(out=out_words[:, :HALF], in_=o_q[:, :HALF].bitcast(I32))
+        for c in range(2, NCH):
             cols = slice(c * CH, (c + 1) * CH)
-            if c == 0:
-                return
-            if c == 1:
-                both = slice(0, 2 * CH)
-                nc.vector.quantize_mx(out=o_q[:, both].bitcast(FP8X4), scales=o_s[:, both], in_=o_b01[:])
-            else:
-                nc.vector.quantize_mx(out=o_q[:, cols].bitcast(FP8X4), scales=o_s[:, cols], in_=o_b[c])
-            if c % 2:
-                done = slice((c - 1) * CH, (c + 1) * CH)
-                nc.sync.dma_start(out=out_words[:, done], in_=o_q[:, done].bitcast(I32))
-
-        hidden_mm(0)
-        for c in range(NCH + 1):
-            if c + 1 < NCH:
-                hidden_mm(c + 1)
-            if c < NCH:
-                leaky(c)
-            if c >= 1:
-                scores(c - 1)
-        for c in range(NCH):
-            message(c)
-        for c in range(NCH):
-            round_out(c)
-        for c in range(NCH):
-            planes(c)
+            quantize(o_q[:, cols], o_s[:, cols], o_b[c][:])
+        nc.sync.dma_start(out=out_words[:, HALF:], in_=o_q[:, HALF:].bitcast(I32))
         for r in range(4):
             queue = nc.scalar if r % 2 else nc.sync
             queue.dma_start(out=out_2[0, r:16:4, :].bitcast(I32), in_=o_s[r:P:32, :].bitcast(I32))

@@ -159,24 +159,20 @@ def tile_picked_zgatt_exp_po_kernel(
         def packed(words, first, t):
             return words[:, 2 * P * t : 2 * P * (t + 1)].bitcast(FP4X4), w_s[:, first + P * t : first + P * (t + 1)]
 
+        v_ps = [psum.tile([P, PACK, CH], F32, name="v_ps%d" % c) for c in range(NCH)]
         small = [sb("small%d" % c, [P, CH * PACK], F32) for c in range(NCH)]
-        h_b01 = sb("h_b01", [P, HALF * PACK], BF16)
-        h_b = [h_b01[:, : CH * PACK], h_b01[:, CH * PACK :]] + [
-            sb("h_b%d" % c, [P, CH * PACK], BF16)[:] for c in range(2, NCH)
+        h_b = [sb("h_b%d" % c, [P, CH * PACK], BF16) for c in range(NCH)]
+        h_q = [sb("h_q%d" % c, [P, CH], U32) for c in range(NCH)]
+        h_s = [sb("h_s%d" % c, [P, CH], U8) for c in range(NCH)]
+        e_f = [sb("e_f%d" % c, [P, PACK, CH], F32) for c in range(NCH)]
+        o_f23 = sb("o_f23", [P, PACK, 2 * CH], F32)
+        o_f = [sb("o_f%d" % c, [P, PACK, CH], F32)[:] for c in range(2)] + [o_f23[:, :, :CH], o_f23[:, :, CH:]]
+        o_b01 = sb("o_b01", [P, 2 * CH * PACK], BF16)
+        o_b = [o_b01[:, : CH * PACK], o_b01[:, CH * PACK :]] + [
+            sb("o_b%d" % c, [P, CH * PACK], BF16)[:] for c in range(2, NCH)
         ]
-        h_q01 = sb("h_q01", [P, HALF], U32)
-        h_s01 = sb("h_s01", [P, HALF], U8)
-        h_q = {c: sb("h_q%d" % c, [P, CH], U32) for c in range(2, NCH)}
-        h_s = {c: sb("h_s%d" % c, [P, CH], U8) for c in range(2, NCH)}
-        e_f = [sb("e_f%d" % c, [P, PACK * CH], F32) for c in range(NCH)]
-        o_f01 = sb("o_f01", [P, PACK, HALF], F32)
-        o_f23 = sb("o_f23", [P, PACK, HALF], F32)
-        o_b01 = sb("o_b01", [P, HALF * PACK], BF16)
-        o_b = {c: sb("o_b%d" % c, [P, CH * PACK], BF16) for c in range(2, NCH)}
         o_q = sb("o_q", [P, S], U32)
         o_s = sb("o_s", [P, S], U8)
-        v_pair = [psum.tile([P, 2, HALF], F32, name="v_pair%d" % u) for u in range(2)]
-        v_ps = {c: psum.tile([P, PACK, CH], F32, name="v_ps%d" % c) for c in range(2, NCH)}
         out_rows = out_0.rearrange("(p t) n -> p t n", t=PACK)
         out_words = out_1[0].rearrange("p n t -> p (n t)").bitcast(I32)
 
@@ -186,103 +182,87 @@ def tile_picked_zgatt_exp_po_kernel(
                 mx(y_ps[c][:, t, :], w2_q[t][:].bitcast(FP8X4), w2_s[t][:], chunk((dst_w0, dst_w1), c),
                    x_s[:, S + c * CH : S + (c + 1) * CH], False, t == order[-1])
 
-        def leaky(c):
-            y_nt = y_ps[c][:].rearrange("p t n -> p n t")
-            small_nt = small[c][:].rearrange("p (n t) -> p n t", t=PACK)
-            nc.scalar.activation(out=small_nt, in_=y_nt, func=ACT.Copy, scale=SLOPE)
-            nc.vector.tensor_tensor(
-                out=h_b[c].rearrange("p (n t) -> p n t", t=PACK), in0=y_nt, in1=small_nt, op=ALU.max
-            )
-
-        def pair_bank(u):
-            return y_ps[u][:].rearrange("p (a b) n -> p a (b n)", a=2)
-
-        def pair_values(u):
-            for a in range(2):
-                mx(v_pair[u][:, a, :], *packed(w4_q, N, 2 * u + a), src_w0[:], x_s[:, :HALF], True, True)
-
-        def chunk_values(c):
+        def values(c):
             for t in range(PACK):
                 mx(v_ps[c][:, t, :], *packed(w4_q, N, t), chunk((src_w0, src_w1), c),
                    x_s[:, c * CH : (c + 1) * CH], True, True)
 
-        def pair_scores(u):
-            for a in range(2):
-                mx(pair_bank(u)[:, a, :], *packed(w3_q, 0, 2 * u + a), h_q01[:], h_s01[:], True, True)
+        def leaky(c):
+            y_nt = y_ps[c][:].rearrange("p t n -> p n t")
             nc.scalar.activation(
-                out=e_f[u][:].rearrange("p (a n) -> p a n", a=2), in_=pair_bank(u), func=ACT.Exp
+                out=small[c][:].rearrange("p (n t) -> p n t", t=PACK), in_=y_nt, func=ACT.Copy, scale=SLOPE
             )
-
-        def pair_message(u):
-            rows = slice(2 * u, 2 * u + 2)
             nc.vector.tensor_tensor(
-                out=o_f01[:, rows], in0=v_pair[u][:], in1=e_f[u][:].rearrange("p (a n) -> p a n", a=2), op=ALU.mult
+                out=h_b[c][:].rearrange("p (n t) -> p n t", t=PACK),
+                in0=y_nt,
+                in1=small[c][:].rearrange("p (n t) -> p n t", t=PACK),
+                op=ALU.max,
             )
-            nc.sync.dma_start(out=out_rows[:, rows, :HALF], in_=o_f01[:, rows])
 
         def score_bank(c, t):
             return y_ps[0] if c == NCH - 1 and t >= PACK // 2 else y_ps[c]
 
-        def chunk_scores(c):
-            quantize(h_q[c][:], h_s[c][:], h_b[c])
+        def scores(c):
+            quantize(h_q[c][:], h_s[c][:], h_b[c][:])
+            if c == NCH - 1:
+                nc.scalar.activation(out=e_f[0][:], in_=y_ps[0][:], func=ACT.Exp)
             for t in range(PACK):
                 mx(score_bank(c, t)[:, t, :], *packed(w3_q, 0, t), h_q[c][:], h_s[c][:], True, True)
 
-        def chunk_message(c):
+        def message(c):
             step = PACK // 2 if c == NCH - 1 else PACK
-            cols = slice((c - 2) * CH, (c - 1) * CH)
-            e_tn = e_f[c][:].rearrange("p (t n) -> p t n", t=PACK)
             for t in range(0, PACK, step):
                 rows = slice(t, t + step)
-                nc.scalar.activation(out=e_tn[:, rows], in_=score_bank(c, t)[:, rows], func=ACT.Exp)
-                nc.vector.tensor_tensor(
-                    out=o_f23[:, rows, cols], in0=v_ps[c][:, rows], in1=e_tn[:, rows], op=ALU.mult
-                )
+                if c > 0:
+                    nc.scalar.activation(out=e_f[c][:, rows], in_=score_bank(c, t)[:, rows], func=ACT.Exp)
+                nc.vector.tensor_tensor(out=o_f[c][:, rows], in0=v_ps[c][:, rows], in1=e_f[c][:, rows], op=ALU.mult)
                 if c == NCH - 1:
-                    nc.sync.dma_start(out=out_rows[:, rows, HALF:], in_=o_f23[:, rows])
+                    nc.sync.dma_start(out=out_rows[:, rows, 2 * CH :], in_=o_f23[:, rows])
+            if c < 2:
+                nc.sync.dma_start(out=out_rows[:, :, c * CH : (c + 1) * CH], in_=o_f[c])
 
-        def round_views(c):
-            cols = slice((c - 2) * CH, (c - 1) * CH)
-            return (
-                o_b[c][:].rearrange("p (n i t) -> p n t i", i=4, t=PACK),
-                o_f23[:, :, cols].rearrange("p t (n i) -> p n t i", i=4),
-            )
+        def round_out(c):
+            dst_v = o_b[c].rearrange("p (n i t) -> p n t i", i=4, t=PACK)
+            src_v = o_f[c].rearrange("p t (n i) -> p n t i", i=4)
+            if c < 2:
+                nc.gpsimd.tensor_scalar(
+                    out=o_b[c].rearrange("p (n t) -> p n t", t=PACK),
+                    in0=o_f[c].rearrange("p t n -> p n t"),
+                    scalar1=1.0, scalar2=-0.0, op0=ALU.mult, op1=ALU.add,
+                )
+            elif c == NCH - 1:
+                nc.vector.tensor_copy(out=dst_v[:, :LAST_VECTOR], in_=src_v[:, :LAST_VECTOR])
+                nc.scalar.copy(out=dst_v[:, LAST_VECTOR:], in_=src_v[:, LAST_VECTOR:])
+            else:
+                nc.scalar.copy(out=dst_v, in_=src_v)
+
+        def planes(c):
+            cols = slice(c * CH, (c + 1) * CH)
+            if c == 0:
+                return
+            if c == 1:
+                both = slice(0, 2 * CH)
+                quantize(o_q[:, both], o_s[:, both], o_b01[:])
+            else:
+                quantize(o_q[:, cols], o_s[:, cols], o_b[c])
+            if c % 2:
+                done = slice((c - 1) * CH, (c + 1) * CH)
+                nc.sync.dma_start(out=out_words[:, done], in_=o_q[:, done].bitcast(I32))
 
         for c in range(NCH):
             close_hidden(c)
-        for u in range(2):
-            pair_values(u)
-        leaky(0)
-        leaky(1)
-        quantize(h_q01[:], h_s01[:], h_b01[:])
-        leaky(2)
-        leaky(3)
-        chunk_values(2)
-        pair_scores(0)
-        pair_scores(1)
-        chunk_values(3)
-        chunk_scores(2)
-        pair_message(0)
-        chunk_scores(3)
-        pair_message(1)
-        nc.gpsimd.tensor_scalar(
-            out=o_b01[:].rearrange("p (n t) -> p n t", t=PACK),
-            in0=o_f01[:].rearrange("p t n -> p n t"),
-            scalar1=1.0, scalar2=-0.0, op0=ALU.mult, op1=ALU.add,
-        )
-        chunk_message(2)
-        chunk_message(3)
-        rounded, exact = round_views(2)
-        nc.scalar.copy(out=rounded, in_=exact)
-        rounded, exact = round_views(3)
-        nc.vector.tensor_copy(out=rounded[:, :LAST_VECTOR], in_=exact[:, :LAST_VECTOR])
-        nc.scalar.copy(out=rounded[:, LAST_VECTOR:], in_=exact[:, LAST_VECTOR:])
-        quantize(o_q[:, :HALF], o_s[:, :HALF], o_b01[:])
-        nc.sync.dma_start(out=out_words[:, :HALF], in_=o_q[:, :HALF].bitcast(I32))
-        for c in range(2, NCH):
-            cols = slice(c * CH, (c + 1) * CH)
-            quantize(o_q[:, cols], o_s[:, cols], o_b[c][:])
-        nc.sync.dma_start(out=out_words[:, HALF:], in_=o_q[:, HALF:].bitcast(I32))
+        for c in range(NCH + 1):
+            if c < NCH:
+                values(c)
+                leaky(c)
+            if c >= 1:
+                scores(c - 1)
+        for c in range(NCH):
+            message(c)
+        for c in range(NCH):
+            round_out(c)
+        for c in range(NCH):
+            planes(c)
         for r in range(4):
             queue = nc.scalar if r % 2 else nc.sync
             queue.dma_start(out=out_2[0, r:16:4, :].bitcast(I32), in_=o_s[r:P:32, :].bitcast(I32))

@@ -24,9 +24,9 @@ HALF = S // 2
 SLOPE = 0.2
 X_ROWS = P - 16
 W_ROWS = P - 32
-W1_VECTOR = 60
+W1_VECTOR = 78
 W2_CUTS = (0, 96, 128)
-W2_VECTOR = (62, 20)
+W2_VECTOR = (68, 22)
 LAST_VECTOR = 16
 W2R_AT, W3_AT, W2A_AT, XS_AT, W4_AT, W2B_AT = 0, 4096, 5120, 11200, 11264, 13184
 W1R_AT = 15360

from contextlib import ExitStack

import concourse.mybir as mybir

K, T, S, H, N = 512, 2048, 512, 512, 512
FLOPS = 2 * (2 * K * H * S + H * N * S + K * N * S)

F32 = mybir.dt.float32
BF16 = mybir.dt.bfloat16
I32 = mybir.dt.int32
U32 = mybir.dt.uint32
U16 = mybir.dt.uint16
U8 = mybir.dt.uint8
FP8X4 = mybir.dt.float8_e4m3fn_x4
FP4X4 = mybir.dt.float4_e2m1fn_x4
ACT = mybir.ActivationFunctionType
ALU = mybir.AluOpType

P = 128
PACK = 4
CH = 128
NCH = S // CH
HALF = S // 2
SLOPE = 0.2
X_ROWS = P - 16
W_ROWS = P - 32
W1_VECTOR = 78
W2_CUTS = (0, 96, 128)
W2_VECTOR = (68, 22)
LAST_VECTOR = 16
W2R_AT, W3_AT, W2A_AT, XS_AT, W4_AT, W2B_AT = 0, 4096, 5120, 11200, 11264, 13184
W1R_AT = 15360


def tile_picked_zgatt_exp_po_kernel(
    tc, x_words, x_scales, w1, w2, w3_words, w3_scales, w4_words, w4_scales, offs, dst, out_0, out_1, out_2
):
    nc = tc.nc
    with ExitStack() as ctx:
        keep = ctx.enter_context(tc.tile_pool(name="keep", bufs=1))
        shared = ctx.enter_context(tc.tile_pool(name="shared", bufs=1))
        psum = ctx.enter_context(tc.psum_pool(name="psum", bufs=1))

        def sb(name, shape, dtype):
            return keep.tile(shape, dtype, name=name, align_bytes=64)

        def at(name, shape, dtype, offset):
            return shared.tile(shape, dtype, name=name, align_bytes=64, offset=offset)

        def mx(out, w, w_scale, x, x_scale, start, stop):
            nc.tensor.matmul_mx(
                out=out, lhsT=w, lhsT_scale=w_scale, rhs=x.bitcast(FP8X4), rhs_scale=x_scale, start=start, stop=stop
            )

        def quantize(words, scales, values):
            nc.vector.quantize_mx(out=words.bitcast(FP8X4), scales=scales, in_=values)

        xs_tab = at("xs_tab", [P, T], U8, XS_AT)
        ws_raw = sb("ws_raw", [P, N], U8)
        x_s = sb("x_s", [P, 2 * S], U8)
        w_s = sb("w_s", [P, 2 * N], U8)
        nc.vector.memset(xs_tab[:X_ROWS, :].bitcast(I32), 0)
        nc.vector.memset(ws_raw[:W_ROWS, :].bitcast(I32), 0)
        nc.vector.memset(x_s[:].bitcast(I32), 0)
        nc.vector.memset(w_s[:].bitcast(I32), 0)

        offs_t = sb("offs_t", [P, S // 16], U16)
        dst_t = sb("dst_t", [P, S // 16], U16)
        nc.sync.dma_start(out=xs_tab[X_ROWS:, :].bitcast(I32), in_=x_scales[0].bitcast(I32))
        nc.sync.dma_start(offs_t[:], offs)
        nc.sync.dma_start(dst_t[:], dst)
        w1_raw = sb("w1_raw", [P, PACK, H], F32)
        nc.sync.dma_start(out=w1_raw[:], in_=w1.rearrange("(p j) c -> p j c", j=PACK))
        for w, rows in enumerate((w3_scales, w4_scales)):
            nc.sync.dma_start(
                out=ws_raw[W_ROWS + w : P : 2, :].bitcast(I32),
                in_=rows[0].bitcast(I32).rearrange("(q r) c -> r q c", r=4),
            )
        xw_tab = sb("xw_tab", [P, T], U32)
        nc.sync.dma_start(out=xw_tab[:].bitcast(I32), in_=x_words[0].rearrange("p n t -> p (n t)").bitcast(I32))

        picked_s = at("picked_s", [P, 2 * S], U8, W3_AT)
        nc.vector.tensor_copy(picked_s[:, :S], xs_tab[:].indirect(offs_t[:]))
        nc.vector.tensor_copy(picked_s[:, S:], xs_tab[:].indirect(dst_t[:]))
        for r in range(4):
            nc.sync.dma_start(out=x_s[r:P:32, :].bitcast(I32), in_=picked_s[X_ROWS + r : P : 4, :].bitcast(I32))

        w2_rows = w2.rearrange("(p j) c -> p j c", j=PACK)
        w2_raw = []
        for h in range(2):
            lo, hi = W2_CUTS[h], W2_CUTS[h + 1]
            piece = at("w2_raw%d" % h, [P, PACK, PACK * (hi - lo)], F32, (W2A_AT, W2B_AT)[h])
            nc.sync.dma_start(out=piece[:], in_=w2_rows[:, :, PACK * lo : PACK * hi])
            w2_raw.append(piece)
        w4_raw = at("w4_raw", [P, 2 * N], U8, W4_AT)
        w3_raw = at("w3_raw", [P, 2 * N], U8, W3_AT)
        nc.sync.dma_start(out=w4_raw[:].bitcast(I32), in_=w4_words[0].bitcast(I32))
        nc.sync.dma_start(out=w3_raw[:].bitcast(I32), in_=w3_words[0].bitcast(I32))

        def round_weight(rounded, raw, lo, cut, hi):
            dealt = rounded[:].rearrange("p (u t m j) -> p u m j t", u=2, t=2, j=PACK)
            rows = raw[:].rearrange("p j (m u t) -> p u m j t", u=2, t=2)
            nc.scalar.copy(out=dealt[:, :, cut:hi], in_=rows[:, :, cut - lo :])
            nc.vector.tensor_copy(out=dealt[:, :, lo:cut], in_=rows[:, :, : cut - lo])

        w1_b = at("w1_b", [P, PACK * H], BF16, W1R_AT)
        w1_q = sb("w1_q", [P, H], U32)
        w1_s = sb("w1_s", [P, H], U8)
        round_weight(w1_b, w1_raw, 0, W1_VECTOR, P)
        quantize(w1_q[:], w1_s[:], w1_b[:])

        ws_dealt = sb("ws_dealt", [P, N], U8)
        nc.vector.tensor_copy(
            out=ws_dealt[:].rearrange("p (t m) -> p t m", t=PACK), in_=ws_raw[:].rearrange("p (m t) -> p t m", t=PACK)
        )
        for r in range(4):
            rows = slice(W_ROWS + 8 * r, W_ROWS + 8 * (r + 1))
            nc.sync.dma_start(out=w_s[r:P:32, :].bitcast(I32), in_=ws_dealt[rows, :].bitcast(I32))

        src_w0 = at("src_w0", [P, HALF], U32, W1R_AT)
        src_w1 = at("src_w1", [P, HALF], U32, W1R_AT + 1024)
        dst_w0 = at("dst_w0", [P, HALF], U32, W1R_AT + 2048)
        y_ps = [psum.tile([P, PACK, CH], F32, name="y_ps%d" % c) for c in range(NCH)]

        def chunk(halves, c):
            return halves[c // 2][:, (c % 2) * CH : (c % 2 + 1) * CH]

        for h, picked in enumerate((src_w0, src_w1)):
            nc.vector.tensor_copy(picked[:], xw_tab[:].indirect(offs_t[:, h * HALF // 16 : (h + 1) * HALF // 16]))
        nc.vector.tensor_copy(dst_w0[:], xw_tab[:].indirect(dst_t[:, : HALF // 16]))
        for c in range(NCH):
            for t in range(PACK):
                m = slice(P * t, P * (t + 1))
                mx(y_ps[c][:, t, :], w1_q[:, m].bitcast(FP8X4), w1_s[:, m], chunk((src_w0, src_w1), c),
                   x_s[:, c * CH : (c + 1) * CH], t == 0, False)

        w2_b = at("w2_b", [P, PACK * H], BF16, W2R_AT)
        w2_q = [sb("w2_q%d" % t, [P, P], U32) for t in range(PACK)]
        w2_s = [sb("w2_s%d" % t, [P, P], U8) for t in range(PACK)]
        for h in range(2):
            lo, hi = W2_CUTS[h], W2_CUTS[h + 1]
            round_weight(w2_b, w2_raw[h], lo, lo + W2_VECTOR[h], hi)
        for t in range(PACK):
            quantize(w2_q[t][:], w2_s[t][:], w2_b[:, PACK * P * t : PACK * P * (t + 1)])
        dst_w1 = at("dst_w1", [P, HALF], U32, W2R_AT)
        nc.vector.tensor_copy(dst_w1[:], xw_tab[:].indirect(dst_t[:, HALF // 16 :]))

        def dealt_words(tile):
            return tile[:].bitcast(U16).rearrange("p (t m) -> p t m", t=PACK)

        def raw_words(tile):
            return tile[:].bitcast(U16).rearrange("p (m t) -> p t m", t=PACK)

        w4_q = at("w4_q", [P, 2 * N], U8, W2B_AT)
        w3_q = at("w3_q", [P, 2 * N], U8, W2R_AT + 1024)
        nc.scalar.copy(out=dealt_words(w4_q), in_=raw_words(w4_raw))
        nc.vector.tensor_copy(out=dealt_words(w3_q), in_=raw_words(w3_raw))

        def packed(words, first, t):
            return words[:, 2 * P * t : 2 * P * (t + 1)].bitcast(FP4X4), w_s[:, first + P * t : first + P * (t + 1)]

        v_ps = [psum.tile([P, PACK, CH], F32, name="v_ps%d" % c) for c in range(NCH)]
        small = [sb("small%d" % c, [P, CH * PACK], F32) for c in range(NCH)]
        h_b = [sb("h_b%d" % c, [P, CH * PACK], BF16) for c in range(NCH)]
        h_q = [sb("h_q%d" % c, [P, CH], U32) for c in range(NCH)]
        h_s = [sb("h_s%d" % c, [P, CH], U8) for c in range(NCH)]
        e_f = [sb("e_f%d" % c, [P, PACK, CH], F32) for c in range(NCH)]
        o_f23 = sb("o_f23", [P, PACK, 2 * CH], F32)
        o_f = [sb("o_f%d" % c, [P, PACK, CH], F32)[:] for c in range(2)] + [o_f23[:, :, :CH], o_f23[:, :, CH:]]
        o_b01 = sb("o_b01", [P, 2 * CH * PACK], BF16)
        o_b = [o_b01[:, : CH * PACK], o_b01[:, CH * PACK :]] + [
            sb("o_b%d" % c, [P, CH * PACK], BF16)[:] for c in range(2, NCH)
        ]
        o_q = sb("o_q", [P, S], U32)
        o_s = sb("o_s", [P, S], U8)
        out_rows = out_0.rearrange("(p t) n -> p t n", t=PACK)
        out_words = out_1[0].rearrange("p n t -> p (n t)").bitcast(I32)

        def close_hidden(c):
            order = list(range(PACK) if c == 0 else reversed(range(PACK)))
            for t in order:
                mx(y_ps[c][:, t, :], w2_q[t][:].bitcast(FP8X4), w2_s[t][:], chunk((dst_w0, dst_w1), c),
                   x_s[:, S + c * CH : S + (c + 1) * CH], False, t == order[-1])

        def values(c):
            for t in range(PACK):
                mx(v_ps[c][:, t, :], *packed(w4_q, N, t), chunk((src_w0, src_w1), c),
                   x_s[:, c * CH : (c + 1) * CH], True, True)

        def leaky(c):
            y_nt = y_ps[c][:].rearrange("p t n -> p n t")
            nc.scalar.activation(
                out=small[c][:].rearrange("p (n t) -> p n t", t=PACK), in_=y_nt, func=ACT.Copy, scale=SLOPE
            )
            nc.vector.tensor_tensor(
                out=h_b[c][:].rearrange("p (n t) -> p n t", t=PACK),
                in0=y_nt,
                in1=small[c][:].rearrange("p (n t) -> p n t", t=PACK),
                op=ALU.max,
            )

        def score_bank(c, t):
            return y_ps[0] if c == NCH - 1 and t >= PACK // 2 else y_ps[c]

        def scores(c):
            quantize(h_q[c][:], h_s[c][:], h_b[c][:])
            if c == NCH - 1:
                nc.scalar.activation(out=e_f[0][:], in_=y_ps[0][:], func=ACT.Exp)
            for t in range(PACK):
                mx(score_bank(c, t)[:, t, :], *packed(w3_q, 0, t), h_q[c][:], h_s[c][:], True, True)

        def message(c):
            step = PACK // 2 if c == NCH - 1 else PACK
            for t in range(0, PACK, step):
                rows = slice(t, t + step)
                if c > 0:
                    nc.scalar.activation(out=e_f[c][:, rows], in_=score_bank(c, t)[:, rows], func=ACT.Exp)
                nc.vector.tensor_tensor(out=o_f[c][:, rows], in0=v_ps[c][:, rows], in1=e_f[c][:, rows], op=ALU.mult)
                if c == NCH - 1:
                    nc.sync.dma_start(out=out_rows[:, rows, 2 * CH :], in_=o_f23[:, rows])
            if c < 2:
                nc.sync.dma_start(out=out_rows[:, :, c * CH : (c + 1) * CH], in_=o_f[c])

        def round_out(c):
            dst_v = o_b[c].rearrange("p (n i t) -> p n t i", i=4, t=PACK)
            src_v = o_f[c].rearrange("p t (n i) -> p n t i", i=4)
            if c < 2:
                nc.gpsimd.tensor_scalar(
                    out=o_b[c].rearrange("p (n t) -> p n t", t=PACK),
                    in0=o_f[c].rearrange("p t n -> p n t"),
                    scalar1=1.0, scalar2=-0.0, op0=ALU.mult, op1=ALU.add,
                )
            elif c == NCH - 1:
                nc.vector.tensor_copy(out=dst_v[:, :LAST_VECTOR], in_=src_v[:, :LAST_VECTOR])
                nc.scalar.copy(out=dst_v[:, LAST_VECTOR:], in_=src_v[:, LAST_VECTOR:])
            else:
                nc.scalar.copy(out=dst_v, in_=src_v)

        def planes(c):
            cols = slice(c * CH, (c + 1) * CH)
            if c == 0:
                return
            if c == 1:
                both = slice(0, 2 * CH)
                quantize(o_q[:, both], o_s[:, both], o_b01[:])
            else:
                quantize(o_q[:, cols], o_s[:, cols], o_b[c])
            if c % 2:
                done = slice((c - 1) * CH, (c + 1) * CH)
                nc.sync.dma_start(out=out_words[:, done], in_=o_q[:, done].bitcast(I32))

        for c in range(NCH):
            close_hidden(c)
        for c in range(NCH + 1):
            if c < NCH:
                values(c)
                leaky(c)
            if c >= 1:
                scores(c - 1)
        for c in range(NCH):
            message(c)
        for c in range(NCH):
            round_out(c)
        for c in range(NCH):
            planes(c)
        for r in range(4):
            queue = nc.scalar if r % 2 else nc.sync
            queue.dma_start(out=out_2[0, r:16:4, :].bitcast(I32), in_=o_s[r:P:32, :].bitcast(I32))
